import numpy as np, ml_dtypes
CORES = [40,41,42,43,44,45,46,47]
N = 8
import mx_ref
BF = ml_dtypes.bfloat16
def gentries(a):
    return np.ascontiguousarray(a.reshape(8, 16, -1).transpose(0, 2, 1)).reshape(8, -1)
def gtable(e):
    e = np.asarray(e); return np.ascontiguousarray(e.reshape(8, -1, 16).transpose(0, 2, 1)).reshape(128, -1).astype(np.int32)
def gcols(t, e):
    v = np.concatenate([t.reshape(8, 16, -1, 4), np.zeros((8, 16, 1, 4), BF)], axis=2)
    return np.ascontiguousarray(np.stack([v[g][:, e[g]] for g in range(8)])).reshape(128, -1)
def tile(rs):
    return np.stack(rs, axis=2).reshape(128, -1).astype(BF)
def pick(q, e):
    c = np.concatenate([q[0].reshape(128, -1, 4), np.zeros((128, 1, 4), np.uint8)], axis=1); s = np.concatenate([q[1], np.ones((16, 1), np.uint8)], axis=1)
    return (np.ascontiguousarray(c[:, e].reshape(128, -1)), np.ascontiguousarray(s[:, e]))
def join(*qs):
    return (np.concatenate([q[0] for q in qs], axis=1), np.concatenate([q[1] for q in qs], axis=1))
def put(q, e, v):
    c, s = q[0].reshape(128, -1, 4).copy(), q[1].copy(); c[:, e] = v[0].reshape(128, -1, 4); s[:, e] = v[1]
    return (c.reshape(128, -1), s)
def pk(c, s):
    return (np.ascontiguousarray(c), mx_ref.live(s))
def emit(q):
    return q[0], q[1]
def packed(v, rng):
    q = [mx_ref.quantize(np.ascontiguousarray(v[r])) for r in range(N)]
    return np.stack([a for a, b in q]), np.stack([mx_ref.plane(b, rng) for a, b in q])
def values_of_codes():
    e, c = np.zeros((128, 128, 4), np.float32), np.zeros((128, 2, 4), np.uint8)
    e[np.arange(128), np.arange(128), 0] = 1
    c[:127, :, 0] = np.arange(256).reshape(2, 128).T[:127]
    return mx_ref.matmul(mx_ref.quantize(e.reshape(128, 512).astype(BF)), (c.reshape(128, 8), np.full((16, 2), 127, np.uint8))).T.reshape(-1).astype(np.float64)
CODE_VALUE, SCALE_VALUE = values_of_codes(), 2.0 ** (np.arange(256) - 127.0)
def decode(q):
    return (CODE_VALUE[q[0]].reshape(16, 8, -1, 4) * SCALE_VALUE[q[1]][:, None, :, None] + 0.0).reshape(128, -1).astype(np.float32)
def f(rng, *shape):
    return mx_ref.flush((rng.standard_normal(shape, dtype=np.float32) * np.exp2(rng.integers(-2, 3, shape[:-1] + (1,)))).astype(BF))
def wide(rng, *shape, cols=0):
    v = rng.standard_normal(shape, dtype=np.float32) * np.exp2(rng.integers(-12, 13, shape)).astype(np.float32)
    if cols: v *= np.repeat(np.exp2(rng.integers(-cols, cols + 1, shape[:-2] + (1, shape[-1] // 4))) * (rng.random(shape[:-2] + (1, shape[-1] // 4)) > 0.0625), 4, axis=-1).astype(np.float32)
    return mx_ref.flush(v.astype(BF))
C, HALF = 320, 160
STEP = [1, 2, 4]
def big(v):
    v = v.astype(np.float32)
    v[np.abs(v) < np.float32(2.0 ** -16)] = 0
    return v.astype(BF)
def numbers_of(rng):
    return {"x": big(f(rng, N, 128, 4 * C)), "u": np.array(f(rng, N, 128, 512)), "v": np.array(f(rng, N, 128, 512))}
def lists(rng):
    e = np.tile(np.arange(C), (N, 8, 1))
    o = rng.permuted(e, axis=2)
    m = np.zeros((N, 8, C), np.int64)
    np.put_along_axis(m, o, o[:, :, np.arange(C) ^ 1], axis=2)
    return rng.permuted(e, axis=2), m
def stored(q, m):
    return {"gq": np.stack([gtable(q[r]) for r in range(N)]), "gm": np.stack([gtable(m[r]) for r in range(N)])}
def layers(rng):
    return big(f(rng, N, 128, 2048)).reshape(N, 8, 16, 4, 8, 16, 4)
def no_layers():
    return np.zeros((N, 8, 16, 4, 8, 16, 4), np.float32)
def weights(rng, w):
    c, p = packed(np.ascontiguousarray(w.astype(BF)).reshape(N, 128, 2048), rng)
    return {"wc": c, "ws": p}
def setup_inputs(rng):
    return {**numbers_of(rng), **stored(*lists(rng)), **weights(rng, layers(rng))}
def setup_inputs_ties(rng):
    d = numbers_of(rng)
    o = rng.permutation(N)
    q, m = lists(rng)
    k = rng.integers(-1, 2, (N, 8, C)).astype(np.float32)
    k[o[0], rng.permutation(8)[:4]] = 0
    k[o[1]] = np.where(rng.permutation(8) < 4, 1, -1)[:, None]
    k[o[3]] = np.where(np.arange(C) < HALF, 1, -3)
    for g in range(8):
        a, b, p = rng.permutation(HALF), HALF + rng.permutation(HALF), rng.permutation(HALF)
        q[o[3], g] = np.concatenate([a, b] if g == 0 else [b, a])
        m[o[3], g, :HALF] = HALF + p
        m[o[3], g, HALF + p] = np.arange(HALF)
    x = d["x"].reshape(N, 8, 16, C, 4)
    x[:, :, 0] = 0
    x[:, :, 0, :, 0] = k.astype(BF)
    u = d["u"].reshape(N, 128, 128, 4)
    u[:, :, ::16] = 0
    for h in range(0, 128, 16): u[:, h, h, 0] = 1
    w = layers(rng)
    w[:, :, :, :, :, 0] = 0
    return {"x": x.reshape(N, 128, 4 * C), "u": u.reshape(N, 128, 512), "v": d["v"], **stored(q, m), **weights(rng, w)}
def setup_inputs_near(rng):
    d = numbers_of(rng)
    o = rng.permutation(N) % 2
    k = np.where(o == 0, 2.0 ** -30, 1.0)
    x = np.zeros((N, 8, 16, C, 4))
    s = rng.integers(-1, 2, (N, 8, C)) * k[:, None, None]
    x[:, :, 0, :, 0] = 1.125 * s
    x[:, :, 1, :, 0] = -1.25 * s
    x[:, :, 7, :, 0] = 2.0 ** -30
    x[:, :, 8, :, 0] = 2.0 ** -30
    for r in range(N):
        at = [0, C - 1, int(rng.integers(C)), int(rng.integers(C))]
        for g, j in zip(rng.permutation(8)[:4], at): x[r, g, 0, j, 0] = 2.0 ** 30 * rng.choice([-1.0, 1.0])
    u = d["u"].reshape(N, 128, 128, 4)
    u[:, :, ::16] = 0
    for h in range(0, 128, 16):
        u[:, h, h, 0] = (1.125 * k).astype(np.float32).astype(BF)
        u[:, h + 1, h, 0] = k.astype(np.float32).astype(BF)
        u[:, h + 9, h, 0] = 2.0 ** -30
    w = no_layers()
    for g in range(8):
        w[:, g, 8, 0, g, 8, 0] = 32
        w[:, g, 1, 0, g, 9, 0] = np.where(o == 0, 2.0 ** -9, 2.0 ** -30)
    return {"x": x.astype(np.float32).reshape(N, 128, 4 * C).astype(BF), "u": u.reshape(N, 128, 512), "v": d["v"], **stored(*lists(rng)), **weights(rng, w)}
def setup_inputs_odd(rng):
    d = numbers_of(rng)
    x = (1.0 + (2 * rng.integers(0, 64, (N, 8, 16, C, 4)) + 1) * 2.0 ** -7) * np.exp2(-rng.integers(0, 7, (N, 8, 16, C, 4)).astype(np.float64)) * rng.choice([-1.0, 1.0], (N, 8, 16, C, 4))
    e = rng.choice([-1.0, 1.0], (N, 8, C)) * 2.0 ** -8
    n = rng.integers(0, 2, (N, 8, C))
    x[:, :, 8:] = 0
    x[:, :, 0, :, 0] = 1.96875 * 2.0 ** 8 * rng.choice([-1.0, 1.0], (N, 8, 1))
    x[:, :, 1, :, 0] = np.where(n == 0, 5.0, 7.0) * e
    x[:, :, 8, :, 0] = np.where(n == 0, -4.5, -7.5) * e
    x[:, :, 10, :, 0] = 1.125 * 2.0 ** -2
    u = d["u"].reshape(N, 128, 128, 4)
    u[:, :, ::16] = 0
    for h in range(0, 128, 16):
        u[:, h + 1, h, 0] = 1
        u[:, h + 8, h, 0] = 1
    w = no_layers()
    for g in range(8):
        w[:, g, 10, 0, g, 9, 0] = 1.75 * 2.0 ** 5
        for b in range(4): w[:, g, 10, b, g, 11:, 0] = rng.choice([1.125, 1.5, 2.0], (N, 5)) * 2.0 ** -9
    return {"x": x.astype(np.float32).reshape(N, 128, 4 * C).astype(BF), "u": u.reshape(N, 128, 512), "v": d["v"], **stored(*lists(rng)), **weights(rng, w)}
def setup_inputs_ends(rng):
    d = numbers_of(rng)
    o, e, h = rng.permutation(N) % 4, rng.permutation(N) % 4, rng.permutation(8)
    s = rng.choice([-1.0, 1.0], (N, 128, C, 4))
    s[o == 0] = -1
    s[o == 1] = rng.choice([-1.0, 1.0], (N, 1, C, 1))[o == 1]
    x = s * (0.955 + 0.02 * rng.random((N, 128, C, 4))) * 2.0 ** 30
    x[o == 3] = 2.0 ** -30
    size = np.where(o == 3, 2.0 ** -30, 2.0 ** 30)
    a = np.stack([rng.permutation(8) % 2 * 2.0 - 1.0 for r in range(N)]) * size[:, None]
    u = d["u"].reshape(N, 128, 128, 4)
    u[:, :, ::16] = a.astype(np.float32).astype(BF)[:, None, :, None]
    v = rng.choice([-1.0, 1.0], (N, 128, 512)) * np.where(o % 2 == 0, 2.0 ** 30, 2.0 ** -30)[:, None, None]
    q, m = lists(rng)
    c = np.arange(C)
    q[e == 0], m[e == 0] = c, C - 1 - c
    q[e == 1], m[e == 1] = C - 1 - c, c ^ 1
    q[e == 2], m[e == 2] = (c + 1) % C, (c + HALF) % C
    w = no_layers()
    i = np.arange(16)
    for r in range(N):
        for b in range(4):
            if o[r] < 3:
                for g in h[:3]: w[r, g, i, b, g, i, b] = -0.125
            w[r, h[4], i, b, h[3], i, b] = 2.0 ** 30 if o[r] == 3 else 2.0 ** -30
    return {"x": x.astype(np.float32).reshape(N, 128, 4 * C).astype(BF), "u": u.reshape(N, 128, 512), "v": v.astype(np.float32).astype(BF), **stored(q, m), **weights(rng, w)}
def setup_inputs_spread(rng):
    d = setup_inputs(rng)
    d["x"] = big(wide(rng, N, 128, 4 * C, cols=6))
    return d
def check_inputs(d):
    b = []
    for k in ("x", "u", "v"):
        a = np.abs(d[k].astype(np.float32))
        if not (np.isfinite(a).all() and ((a == 0) | (a >= 2.0 ** -30) & (a <= 2.0 ** 30)).all()): b.append("a value of " + k)
    none, least, most = [emit(mx_ref.quantize(np.full((128, 16), k, np.float32).astype(BF)))[1][0, 0] for k in (0.0, 2.0 ** -30, 2.0 ** 30)]
    c = np.arange(C)
    for r in range(N):
        if not (np.sort(gentries(d["gq"][r]), axis=1) == c).all(): b.append("gq: not each column once in a group")
        m = gentries(d["gm"][r])
        if not ((m >= 0) & (m < C)).all(): b.append("an entry of gm")
        elif not ((np.take_along_axis(m, m, axis=1) == c) & (m != c)).all(): b.append("gm: not pairs")
        if ((d["wc"][r] == 0x7F) | (d["wc"][r] == 0xFF)).any(): b.append("wc: a code that is no number")
        s = mx_ref.live(d["ws"][r])
        if ((s != none) & ((s < least) | (s > most))).any(): b.append("ws: a scale out of range")
        if (((d["wc"][r].reshape(16, 8, 512, 4) & 0x7F) != 0) & (s == none)[:, None, :, None]).any(): b.append("wc: a code other than zero under the scale of zeros")
    return b
def exchange(s, m):
    bit = np.roll(s[::16] > 0, 1, axis=0)
    return np.where(np.take_along_axis(bit, np.minimum(m, np.arange(C)), axis=1), m, np.arange(C))
def reference(x, u, v, gq, gm, wc, ws):
    qu = [mx_ref.quantize(u[r]) for r in range(N)]
    lay = [pk(wc[r], ws[r]) for r in range(N)]
    kept, pair = [gentries(gq[r]) for r in range(N)], [gentries(gm[r]) for r in range(N)]
    now = [x[r] for r in range(N)]
    for step in STEP:
        mid, back, sent = [], [], []
        for r in range(N):
            q, m = kept[r], pair[r]
            a, b = np.zeros((9, C), np.int64), np.zeros((9, C), np.int64)
            go = exchange(mx_ref.matmul(qu[r], mx_ref.quantize(now[r])), m)
            a[0] = np.arange(C)
            for g in range(8): a[g + 1] = q[g][go[g][a[g]]]
            t = ((now[r].astype(np.float32) + gcols(now[r], a[1:]).astype(np.float32)) * np.float32(0.5)).astype(BF)
            qt = mx_ref.quantize(t)
            go = exchange(mx_ref.matmul(qu[r], qt), m)
            inv = np.argsort(q, axis=1)
            b[8] = a[8]
            for g in range(7, -1, -1): b[g] = go[g][inv[g][b[g + 1]]]
            sent.append(mx_ref.quantize(tile([mx_ref.matmul(pick(lay[r], np.arange(128 * k, 128 * k + 128)), qt) * np.float32(0.03125) for k in range(4)])))
            miss = np.take_along_axis(a[:8] != b[:8], np.minimum(m, np.arange(C)), axis=1)
            kept[r] = np.where(miss, np.take_along_axis(q, m, axis=1), q)
            mid.append(t)
            back.append(b[:8])
        now = [(mid[r].astype(np.float32) + gcols(decode(sent[r ^ step]).astype(BF), back[r]).astype(np.float32)).astype(BF) for r in range(N)]
    y, qo = np.zeros((N, 128, C), np.float32), np.zeros((N, 8, C), np.float32)
    oc, osc = np.zeros((N, 128, 4 * C), np.uint8), np.zeros((N, 16, C), np.uint8)
    for r in range(N):
        q = mx_ref.quantize(now[r])
        y[r] = mx_ref.matmul(mx_ref.quantize(v[r]), q)
        qo[r] = kept[r]
        oc[r], osc[r] = emit(q)
    return {"y": y, "qo": qo, "oc": oc, "osc": osc}

@@ -1,0 +1,498 @@
+from concourse.mybir import dt, AluOpType as A, ActivationFunctionType as F
+
+C = 320
+ROUNDS = (1, 2, 4)
+HALVES = ((0, 160), (160, 320))
+EPS = 2.0 ** -93
+
+SCRATCH = {}
+
+
+def _buf(dtype, **widths):
+    for k, n in widths.items():
+        SCRATCH[k] = ("sbuf", [128, n], dtype)
+
+
+_buf("bfloat16", xt=1280, xn0=1280, xn1=1280, xn2=1280, xp=1280, xi=1280, vt=1280, ht=1280, dp=1280, ut=512, vv=512, et=2048, ones=512,
+     iot=320, j16=320, df=320, ha=320, hb=320, hc=320, tw=64, qr=320, qmr=320, qir=320, mr=320, mqr=320, d0f=1280, d1f=1280, d0b=1280, d1b=1280,
+     tf=640, tb=640, w0=640, w1=640, zs=128, zt=192, sw=160, e1=128, e2=128, e3=128, e4=128, lf1=128, lf2=128, lb1=128, lb2=128,
+     sg0=320, sg1=320, frf=1600, frb=1600, tt=320, rr=160, rr8=160, mm=320, tm=320, ac=32, at=32, a2=32, bc=32, bt=32, md=32, cu0=64, cu1=64, cut=64)
+_buf("float32", ktm=40, ktn=40, ie=20, col=8, iwc=20, vf=10, qf=20, mf=20, qmw=20, qiw=20, mqw=20, wm=320, qout=640, yt=320)
+_buf("int32", icol=4, gqs=20, gms=20)
+_buf("uint16", offu=16, qo16=20, mo16=20, qio=20, kof=40, kob=40, lof=40, hif=40, tif=40, hib=40, tib=40, fl=20, sl=10, slb=10, ll=20, llb=20, xo=20, xob=20, moff=80, ktf=40, ktb=40)
+for _n, _w in (("uq", 128), ("us", 256), ("xq", 320), ("vq", 320), ("vvq", 128), ("eq", 512), ("wq", 512), ("hq", 960), ("rq", 960)):
+    SCRATCH[_n + "c"] = ("sbuf", [128, _w], "float8_e4m3fn_x4")
+    SCRATCH[_n + "s"] = ("sbuf", [128, _w], "uint8")
+for _b in range(8):
+    SCRATCH["ps%d" % _b] = ("psum", [128, 512], "float32")
+
+NDMA = 20
+SEMAPHORES = ["qv", "qs", "qt", "qg", "lsem"] + ["d%d" % i for i in range(NDMA)] + ["ar%d_%d" % (r, h) for r in range(3) for h in range(2)]
+
+PLACE = {"kf": ("col", 0, 1), "mo": ("col", 1, 1), "me": ("col", 2, 1), "hh": ("col", 3, 1), "ca": ("col", 4, 1), "p31f": ("col", 5, 1),
+         "pi": ("icol", 0, 1), "ki": ("icol", 1, 1), "si": ("icol", 2, 1), "p31": ("icol", 3, 1),
+         "tw1": ("tw", 0, 16), "tw2": ("tw", 32, 32)}
+
+
+def R(name, c0=0, c1=None, st=1, p0=0, p1=128):
+    if name in PLACE:
+        name, at, n = PLACE[name]
+        return (name, at + c0, at + (n if c1 is None else c1), st, p0, p1)
+    return (name, c0, SCRATCH[name][1][1] if c1 is None else c1, st, p0, p1)
+
+
+def half(name, l, n=640):
+    return R(name, n * l, n * l + n)
+
+
+def rank_program(g, core, T, topo):
+    rank = T.rank_of(core)
+    if rank is None:
+        return
+    queue = {"v": g.vector, "s": g.scalar, "t": g.tensor, "g": g, "y": g.sync}
+    count = {"qv": 0, "qs": 0, "qt": 0, "qg": 0}
+    known = {k: {} for k in queue}
+    clock = {}
+    writes, reads = {}, {}
+    pending = {}
+    state = {"bank": 0, "dma": 0}
+
+    def ap(r):
+        name, c0, c1, st, p0, p1 = r
+        return T[name][p0:p1, c0:c1:st] if st > 1 else T[name][p0:p1, c0:c1]
+
+    def hit(a, b):
+        if a[4] >= b[5] or b[4] >= a[5] or a[1] >= b[2] or b[1] >= a[2]:
+            return False
+        return not (a[3] == b[3] and a[3] > 1 and (a[1] - b[1]) % a[3])
+
+    def inside(a, b):
+        return a[4] >= b[4] and a[5] <= b[5] and a[1] >= b[1] and a[2] <= b[2] and (b[3] == 1 or (a[3] == b[3] and (a[1] - b[1]) % a[3] == 0))
+
+    def settle(q, events):
+        for sem, val in sorted(events, key=lambda e: (-len(clock[e]), e[0], -e[1])):
+            if known[q].get(sem, 0) < val:
+                queue[q].wait_ge(T.sem[sem], val)
+                for s, v in clock[(sem, val)].items():
+                    known[q][s] = max(known[q].get(s, 0), v)
+                known[q][sem] = val
+
+    def order(q, outs, ins):
+        ev = set()
+        for r in ins:
+            ev |= {e for w, e in writes.get(r[0], []) if hit(r, w)}
+        for r in outs:
+            ev |= {e for w, e in writes.get(r[0], []) if hit(r, w)}
+            ev |= {e for w, e in reads.get(r[0], []) if hit(r, w) and e[0] != "q" + q}
+        settle(q, ev)
+
+    def note(outs, ins, ev):
+        for r in outs:
+            for book in (writes, reads):
+                book[r[0]] = [(w, e) for w, e in book.get(r[0], []) if not inside(w, r)]
+            writes[r[0]].append((r, ev))
+        for r in ins:
+            reads.setdefault(r[0], []).append((r, ev))
+
+    def op(q, outs, ins, fn):
+        order(q, outs, ins)
+        sem = "q" + q
+        clk = dict(known[q])
+        fn().then_inc(T.sem[sem], 1)
+        count[sem] += 1
+        clk[sem] = count[sem]
+        clock[(sem, count[sem])] = clk
+        note(outs, ins, (sem, count[sem]))
+
+    def dma(q, outs, ins, dst, src):
+        order(q, outs, ins)
+        sem = "d%d" % state["dma"]
+        state["dma"] += 1
+        clock[(sem, 16)] = dict(known[q])
+        queue[q].dma_start(dst, src).then_inc(T.sem[sem], 16)
+        pending[sem] = 16
+        note(outs, ins, (sem, 16))
+
+    def copy(out, src):
+        op("v", [out], [src], lambda: g.vector.tensor_copy(ap(out), ap(src)))
+
+    def pick(q, out, win, off):
+        if q == "v":
+            op(q, [out], [win, off], lambda: g.vector.tensor_copy(ap(out), ap(win).indirect(ap(off))))
+        else:
+            op(q, [out], [win, off], lambda: g.scalar.activation(ap(out), ap(win).indirect(ap(off)), F.Copy))
+
+    def pick_tt(out, win, off, other, alu):
+        op("v", [out], [win, off, other], lambda: g.vector.tensor_tensor(ap(out), ap(win).indirect(ap(off)), ap(other), alu))
+
+    def ts(out, src, s1, op0, s2=None, op1=None):
+        col = [s for s in (s1, s2) if isinstance(s, tuple)]
+        a1 = ap(s1) if isinstance(s1, tuple) else s1
+        a2 = ap(s2) if isinstance(s2, tuple) else s2
+        if op1 is None:
+            op("v", [out], [src] + col, lambda: g.vector.tensor_scalar(ap(out), ap(src), a1, None, op0))
+        else:
+            op("v", [out], [src] + col, lambda: g.vector.tensor_scalar(ap(out), ap(src), a1, a2, op0, op1))
+
+    def tt(out, a, b, alu):
+        op("v", [out], [a, b], lambda: g.vector.tensor_tensor(ap(out), ap(a), ap(b), alu))
+
+    def fill(out, val):
+        op("v", [out], [], lambda: g.vector.memset(ap(out), val))
+
+    def iota(out, pattern, base, cm):
+        op("g", [out], [], lambda: g.iota(ap(out), pattern, base, cm, allow_small_or_imprecise_dtypes=True))
+
+    def turn(out, src):
+        op("v", [out], [src], lambda: g.vector.transpose(ap(out), ap(src)))
+
+    def scan(out, d0, d1, op0, op1):
+        op("v", [out], [d0, d1], lambda: g.vector.tensor_tensor_scan(ap(out), ap(d0), ap(d1), 0.0, op0, op1))
+
+    def quant(name, src, c0, c1):
+        o, s = R(name + "c", c0, c1), R(name + "s", c0, c1)
+        op("v", [o, s], [src], lambda: g.vector.quantize_mx(ap(o), ap(s), ap(src)))
+
+    def mx(bank, n, wname, w0, mname, m0):
+        w, ws, m, ms = R(wname + "c", w0, w0 + 128), R(wname + "s", w0, w0 + 128), R(mname + "c", m0, m0 + n), R(mname + "s", m0, m0 + n)
+        o = R("ps%d" % bank, 0, n)
+        op("t", [R("ps%d" % bank)], [w, ws, m, ms], lambda: g.tensor.matmul_mx(ap(o), ap(w), ap(ws), ap(m), ap(ms), True, True))
+
+    def act(out, src, func, scale=1.0, bias=0.0):
+        op("s", [out], [src], lambda: g.scalar.activation(ap(out), ap(src), func, bias=bias, scale=scale))
+
+    def wrap(src):
+        scan(R("wm"), R("hc"), src, A.add, A.max)
+        return R("wm", 15, 320, 16)
+
+    waiting = []
+
+    def spare(n=1):
+        for _ in range(n):
+            if waiting:
+                waiting.pop(0)()
+
+    dma("y", [R("gqs")], [], ap(R("gqs")), T.gq[:, :])
+    dma("y", [R("gms")], [], ap(R("gms")), T.gm[:, :])
+    dma("y", [R("xt")], [], ap(R("xt")), T.x[:, :])
+    dma("s", [R("ut")], [], ap(R("ut")), T.u[:, :])
+    order("y", [], [R("xt")])
+    dma("y", [R("wqc")], [], T.wqc[:, :].bitcast(dt.uint8), T.wc[:, :])
+    dma("y", [R("wqs")], [], T.wqs[:, :], T.ws[:, :])
+    dma("y", [R("vv")], [], ap(R("vv")), T.v[:, :])
+
+    def one(n):
+        return R(n, 0, 1)
+
+    def bits(out, s1, op0, s2=None, op1=None):
+        if op1 is None:
+            op("v", [one(out)], [one("pi")], lambda: g.vector.tensor_scalar(ap(one(out)), ap(one("pi")), s1, None, op0))
+        else:
+            op("v", [one(out)], [one("pi")], lambda: g.vector.tensor_scalar(ap(one(out)), ap(one("pi")), s1, s2, op0, op1))
+    op("g", [one("pi")], [], lambda: g.iota(ap(one("pi")), [[0, 1]], 0, 1))
+    iota(R("ie"), [[16, 20]], 0, 0)
+    iota(R("j16"), [[0, 20], [1, 16]], 0, 0)
+    iota(R("iot"), [[1, C]], -160, 0)
+    iota(R("d0f"), [[0, 1280]], 1024, 0)
+    iota(R("ones"), [[0, 512]], 1, 0)
+    for b in range(4):
+        o = R("et", 512 * b, 512 * b + 512)
+        op("g", [o], [R("ones")], lambda o=o, b=b: g.affine_select(ap(o), ap(R("ones")), [[-1, 512]], A.is_equal, 0.0, b, 4))
+    iota(R("d0b"), [[0, 1280]], 1024, 0)
+    for e in range(8):
+        q, l = e % 4, e // 4
+        fill(R("offu", 2 * e, 2 * e + 2), 16 * ((2 * q + l + 7) % 8))
+    bits("ki", 15, A.bitwise_and)
+    bits("si", 4, A.arith_shift_right, 1, A.bitwise_and)
+    bits("p31", 31, A.bitwise_and)
+    copy(one("kf"), one("ki"))
+    copy(one("mo"), one("si"))
+    copy(one("p31f"), one("p31"))
+    ts(one("hh"), one("kf"), 15.0, A.is_lt, 512.0, A.mult)
+    ts(one("me"), one("mo"), -1.0, A.mult, 1.0, A.add)
+    ts(R("df"), R("j16"), one("kf"), A.subtract)
+    ts(one("ca"), one("hh"), 160.5, A.subtract)
+    ts(R("ha"), R("df"), 0.0, A.is_equal, -4096.0, A.mult)
+    ts(R("hb"), R("df"), 1.0, A.is_equal, 512.0, A.mult)
+    ts(R("iwc"), R("ie"), one("kf"), A.add, 160.0, A.subtract)
+    fill(R("zs"), 0.0)
+
+    copy(R("qo16"), R("gqs"))
+    copy(R("mo16"), R("gms"))
+    pick("v", R("qr"), R("iot"), R("qo16"))
+    ts(R("qf"), R("gqs"), 160.0, A.subtract)
+    ts(R("mf"), R("gms"), 160.0, A.subtract)
+    pick("v", R("qmr"), R("qr"), R("mo16"))
+    tt(R("zs", 0, 20), R("iwc"), R("mf"), A.min)
+    tt(R("hc"), R("ha"), R("hb"), A.add)
+    fill(R("tw1", 0, 1), -512.0)
+    w = wrap(R("qmr"))
+    quant("uq", R("ut"), 0, 128)
+    ts(R("qmw"), w, one("hh"), A.subtract)
+    op("s", [R("uss")], [R("uqs"), R("offu")], lambda: g.scalar.activation(T.uss[:, 0:256], T.uqs[:, 0:128].indirect(T.offu[:, 0:16]), F.Copy))
+    pick("s", R("mr"), R("iot"), R("mo16"))
+    fill(R("zt"), 0.0)
+    tt(R("zs", 32, 52), R("qf"), R("qmw"), A.min)
+    tt(R("zs", 64, 84), R("qf"), R("qmw"), A.max)
+    tt(R("zs", 96, 116), R("qmw"), R("qf"), A.is_gt)
+    fill(R("tw1", 1, 16), 512.0)
+
+    def spread(o1, o2):
+        return [lambda: turn(R("zt", 32, 160), R("zs")),
+                lambda: ts(R("e1"), R("zs"), one("me"), A.mult),
+                lambda: ts(R("e3"), R("zs"), one("mo"), A.mult),
+                lambda: turn(R("sw"), R("zt", 16, 176)),
+                lambda: ts(R("e2"), R("sw", 0, 128), one("mo"), A.mult),
+                lambda: ts(R("e4"), R("sw", 32, 160), one("me"), A.mult),
+                lambda: tt(R(o1), R("e1"), R("e2"), A.add),
+                lambda: tt(R(o2), R("e3"), R("e4"), A.add)]
+
+    def offs(name, l, slot, add):
+        ts(half(name, l, 20), R("l%s%d" % (name[2], l + 1), 32 * slot, 32 * slot + 20), add, A.add)
+
+    for f in spread("lf1", "lf2"):
+        f()
+    offs("tif", 0, 3, 0.0)
+    offs("hif", 0, 2, 160.0)
+    pick("s", half("tf", 0, 320), R("tw1"), half("tif", 0, 20))
+    op("v", [R("usc")], [R("uqc"), R("offu")], lambda: g.vector.tensor_copy(T.usc[:, 0:256].bitcast(dt.uint32), T.uqc[:, 0:128].bitcast(dt.uint32).indirect(T.offu[:, 0:16])))
+    quant("xq", R("xt"), 0, C)
+    offs("kof", 0, 0, 160.0)
+    offs("lof", 0, 1, 160.0)
+    pick("s", R("d0f", 1, 640, 2), R("iot"), half("lof", 0, 20))
+
+    def signs(l, moving):
+        mx(l, C, "us", 128 * l, moving, 0)
+        act(R("sg%d" % l), R("ps%d" % l, 0, C), F.Sign, bias=-EPS)
+
+    def ring():
+        state["bank"] += 1
+        return 2 + state["bank"] % 6
+
+    signs(0, "xq")
+    signs(1, "xq")
+    pick("v", R("d1f", 1, 640, 2), R("iot"), half("hif", 0, 20))
+    for n, slot, add in (("tif", 3, 0.0), ("hif", 2, 160.0), ("kof", 0, 160.0), ("lof", 1, 160.0)):
+        offs(n, 1, slot, add)
+    pick("s", half("tf", 1, 320), R("tw1"), half("tif", 1, 20))
+    pick("s", R("d1f", 641, 1280, 2), R("iot"), half("hif", 1, 20))
+    pick("s", R("d0f", 641, 1280, 2), R("iot"), half("lof", 1, 20))
+
+    def choose(d, l):
+        pick_tt(R("d1" + d, 640 * l, 640 * l + 640, 2), R("sg%d" % l), half("ko" + d, l, 20), half("t" + d, l, 320), A.mult)
+
+    def rows(d, l):
+        scan(half("fr" + d, l), half("d0" + d, l), half("d1" + d, l), A.max, A.min)
+
+    def lists(d, q, src, st, with_sl):
+        s = R("tt", 0, 10 * st, st, 32 * src, 32 * src + 32)
+        sl, ll = ("sl", "ll") if d == "f" else ("slb", "llb")
+        p = (32 * q, 32 * q + 32)
+        if with_sl == 1:
+            ts(R(sl, 0, 10, 1, *p), s, 160.0, A.add)
+        if d == "f":
+            ts(R(ll, 0, 20, 2, *p), s, 160.5, A.add, 2.0, A.mult)
+            ts(R(ll, 1, 20, 2, *p), s, 1440.0, A.add)
+        else:
+            ts(R(ll, 0, 20, 2, *p), s, 1440.0, A.add)
+            ts(R(ll, 1, 20, 2, *p), s, 480.5, A.add, 2.0, A.mult)
+        if with_sl == 2:
+            ts(R(sl, 0, 10, 1, *p), s, 160.0, A.add)
+
+    def step(d, q, to, with_sl):
+        pick("v", R("rr"), R("fr" + d, 1280, 1600), R("sl" if d == "f" else "slb"))
+        spare()
+        turn(R("tt", 0, 160, 1, 32 * q, 32 * q + 32), R("rr", 0, 160, 1, 32 * q, 32 * q + 32))
+        spare()
+        lists(d, to, q, 16, with_sl)
+
+    def finish(d, out, crossed):
+        pick("v", R("mm"), R("fr" + d), R("ll" if d == "f" else "llb"))
+        spare()
+        turn(R("tm"), R("mm"))
+        spare()
+        ts(R(out), R("tm", 0, 320, 16), 160.0, A.add)
+        spare()
+        for q in crossed:
+            p = (32 * q, 32 * q + 32)
+            ts(R(out, 1, 20, 4, *p), R("tm", 32, 320, 64, *p), 160.0, A.add)
+            ts(R(out, 2, 20, 4, *p), R("tm", 16, 320, 64, *p), 160.0, A.add)
+
+    def compose(d, first):
+        w = wrap(R("fr" + d, 640 * first + 1, 640 * first + 640, 2))
+        rows(d, 1 - first)
+        ts(R("fl"), w, one("ca"), A.subtract, 2.0, A.mult)
+        spare()
+        pick("v", R("fr" + d, 1280, 1600), half("fr" + d, 1 - first), R("fl"))
+
+    def planes(src):
+        for t in range(4):
+            act(R("xp", C * t, C * t + C), R(src, t, 1280, 4), F.Copy, scale=0.5)
+        act(R("xi"), R(src), F.Copy, scale=0.5)
+
+    planes("xt")
+    ts(R("vf"), R("ie", 0, 10), 2.0, A.mult, one("p31f"), A.add)
+    waiting += [
+        lambda: op("v", [R("qir")], [R("qo16"), R("iot")], lambda: g.vector.tensor_copy(ap(R("qir")).indirect(ap(R("qo16"))), ap(R("iot")))),
+        lambda: ts(R("qiw"), wrap(R("qir")), one("hh"), A.subtract),
+        lambda: ts(R("qio"), R("qiw"), 160.0, A.add),
+        lambda: pick("s", R("mqr"), R("mr"), R("qio")),
+        lambda: ts(R("mqw"), wrap(R("mqr")), one("hh"), A.subtract),
+        lambda: (tt(R("zs", 32, 52), R("qiw"), R("mqw"), A.min), tt(R("zs", 64, 84), R("qiw"), R("mqw"), A.max), tt(R("zs", 96, 116), R("mqw"), R("qiw"), A.is_gt))]
+    waiting += spread("lb1", "lb2")
+
+    def back_offs(l):
+        for n, slot, add in (("tib", 3, 0.0), ("hib", 2, 160.0), ("kob", 1, 160.0)):
+            offs(n, l, slot, add)
+        pick("s", half("tb", l, 320), R("tw1"), half("tib", l, 20))
+        pick("s", R("d1b", 640 * l + 1, 640 * l + 640, 2), R("iot"), half("hib", l, 20))
+        pick("s", R("d0b", 640 * l + 1, 640 * l + 640, 2), R("iot"), half("kob", l, 20))
+    waiting += [lambda: back_offs(1), lambda: back_offs(0)]
+    copy(R("sl"), R("vf"))
+    ts(R("ll", 0, 20, 2), R("vf"), 2.0, A.mult, 1.0, A.add)
+    ts(R("ll", 1, 20, 2), R("vf"), 1280.0, A.add)
+
+    def leftover():
+        copy(R("slb"), R("vf"))
+        ts(R("llb", 0, 20, 2), R("vf"), 1280.0, A.add)
+        ts(R("llb", 1, 20, 2), R("vf"), 2.0, A.mult, 641.0, A.add)
+        for n in ("ac", "bc"):
+            fill(R(n), 0.0)
+        for c0, c1, v in ((0, 1, 512.0), (1, 16, -512.0), (16, 17, -512.0), (17, 32, 512.0)):
+            fill(R("tw2", c0, c1), v)
+        copy(R("ac", 0, 20), R("iwc"))
+        quant("eq", R("et"), 0, 512)
+        turn(R("at"), R("ac"))
+        quant("vvq", R("vv"), 0, 128)
+        copy(R("a2", 0, 16, 1, 0, 32), R("at", 0, 16, 1, 0, 32))
+
+    def window_lists():
+        res = []
+        for d, slot in (("f", 0), ("b", 1)):
+            res += [lambda d=d, l=l: ts(half("ktm", l, 20), R("l%s%d" % (d, l + 1), 96, 116), -320.0, A.mult, 480.0, A.add) for l in range(2)]
+            res += [lambda d=d, l=l, slot=slot: tt(half("ktn", l, 20), half("ktm", l, 20), R("l%s%d" % (d, l + 1), 32 * slot, 32 * slot + 20), A.add) for l in range(2)]
+            res += [lambda d=d: copy(R("kt" + d), R("ktn"))]
+        return res
+
+    for rnd, s in enumerate(ROUNDS):
+        peer = T.cores[rank ^ s]
+        rid, pid, _se = topo.addr(peer)
+        mask, neng = topo.mask(core, peer), len(topo.engines(core, peer))
+        choose("f", 0)
+        choose("f", 1)
+        rows("f", 0)
+        compose("f", 0)
+        spare()
+        turn(R("tt", 0, 320, 1, 0, 32), R("frf", 1280, 1600, 1, 0, 32))
+        spare()
+        lists("f", 1, 0, 32, 1)
+        step("f", 1, 2, 1)
+        step("f", 2, 3, 2)
+        finish("f", "xo", (2,))
+        while waiting:
+            spare()
+        for t in range(4):
+            pick_tt(R("vt", t, 1280, 4), R("xp", C * t, C * t + C), R("xo"), R("xi", t, 1280, 4), A.add)
+        quant("vq", R("vt"), 0, C)
+        signs(1, "vq")
+        signs(0, "vq")
+        for h, (c0, c1) in enumerate(HALVES):
+            for b in range(4):
+                k = ring()
+                mx(k, c1 - c0, "wq", 128 * b, "vq", c0)
+                act(R("ht", 4 * c0 + b, 4 * c1, 4), R("ps%d" % k, 0, c1 - c0), F.Copy, scale=0.03125)
+        if rnd == 0:
+            leftover()
+        pick("v", R("rr8"), R("frf", 1280, 1600), R("sl"))
+        ts(R("ac", 0, 20), R("xo"), 160.0, A.subtract)
+        turn(R("tt", 0, 160, 1, 96, 128), R("rr8", 0, 160, 1, 96, 128))
+        turn(R("at"), R("ac"))
+        lists("b", 3, 3, 16, 1)
+        copy(R("a2", 16, 32), R("at", 0, 16))
+        for q in range(3):
+            copy(R("a2", 0, 16, 1, 32 * q + 32, 32 * q + 64), R("at", 16, 32, 1, 32 * q, 32 * q + 32))
+
+        def send(h):
+            c0, c1 = C * rnd + HALVES[h][0], C * rnd + HALVES[h][1]
+            quant("hq", R("ht", 4 * HALVES[h][0], 4 * HALVES[h][1]), c0, c1)
+            order("g", [], [R("hqc", c0, c1), R("hqs", c0, c1)])
+            sem = "ar%d_%d" % (rnd, h)
+            g.remote_dma(T.rqc[:, c0:c1].bitcast(dt.uint8), T.hqc[:, c0:c1].bitcast(dt.uint8), T.sem[sem], T.sem.lsem, pid, rid, mask)
+            g.remote_dma(T.rqs[:, c0:c1], T.hqs[:, c0:c1], T.sem[sem], T.sem.lsem, pid, rid, mask)
+            pending["lsem"] = pending.get("lsem", 0) + 2 * neng
+            pending[sem] = 2 * neng
+            clock[(sem, 2 * neng)] = {}
+            note([R("rqc", c0, c1), R("rqs", c0, c1)], [], (sem, 2 * neng))
+
+        choose("b", 1)
+        choose("b", 0)
+        send(0)
+        rows("b", 1)
+        send(1)
+        if rnd == 0:
+            waiting += window_lists()
+        compose("b", 1)
+        spare()
+        step("b", 3, 2, 1)
+        step("b", 2, 1, 1)
+        step("b", 1, 0, 0)
+        for h, (c0, c1) in enumerate(HALVES):
+            for b in range(4):
+                k = ring()
+                mx(k, c1 - c0, "eq", 128 * b, "rq", C * rnd + c0)
+                act(R("dp", C * b + c0, C * b + c1), R("ps%d" % k, 0, c1 - c0), F.Copy)
+        finish("b", "xob", (1, 3))
+        while waiting:
+            spare()
+        xn = "xn%d" % rnd
+
+        def part(t):
+            pick_tt(R(xn, t, 1280, 4), R("dp", C * t, C * t + C), R("xob"), R("vt", t, 1280, 4), A.add)
+
+        def tables(d, l):
+            pick("s", half("t" + d, l, 320) if rnd < 2 else R("d1f", 640 * l, 640 * l + 640, 2), R("w%d" % l), half("kt" + d, l, 20))
+        ts(R("bc", 0, 20), R("xob"), 160.0, A.subtract)
+        part(0)
+        turn(R("bt"), R("bc"))
+        cu, old = "cu%d" % (rnd % 2), "cu%d" % (1 - rnd % 2)
+        pairs = ((16, 48, 0, 32), (0, 16, 0, 16), (48, 64, 16, 32))
+        if rnd == 0:
+            for c0, c1, m0, m1 in pairs:
+                tt(R(cu, c0, c1), R("a2", m0, m1), R("bt", m0, m1), A.not_equal)
+        else:
+            tt(R("md"), R("a2"), R("bt"), A.not_equal)
+            for c0, c1, m0, m1 in pairs:
+                tt(R(cu, c0, c1), R(old, 16 + m0, 16 + m1), R("md", m0, m1), A.not_equal)
+        turn(R("cut"), R(cu))
+        for l in range(2):
+            for k in range(2):
+                ts(R("moff", 40 * l + 20 * k, 40 * l + 20 * k + 20), R("cut", 32 * l, 32 * l + 20), 16.0 * (k if rnd < 2 else 1 - k), A.add)
+        pick("s", R("w0"), R("tw2"), half("moff", 0, 40))
+        tables("f", 0)
+        pick("s", R("w1"), R("tw2"), half("moff", 1, 40))
+        for t in (1, 2, 3):
+            part(t)
+        quant("xq", R(xn), 0, C)
+        if rnd < 2:
+            signs(0, "xq")
+            tables("f", 1)
+            signs(1, "xq")
+            planes(xn)
+            tables("b", 1)
+            tables("b", 0)
+
+    mx(0, C, "vvq", 0, "xq", 0)
+    dma("y", [], [R("xqc")], T.oc[:, :], T.xqc[:, :].bitcast(dt.uint8))
+    for k in range(4):
+        dma("y", [], [R("xqs")], T.osc[4 * k:4 * k + 4, :], T.xqs[32 * k:32 * k + 4, :])
+    act(R("yt"), R("ps0", 0, C), F.Copy)
+    dma("s", [], [R("yt")], T.y[:, :], ap(R("yt")))
+    tables("f", 1)
+    for l in range(2):
+        rows("f", l)
+        act(half("qout", l, 320), R("frf", 640 * l + 1, 640 * l + 640, 2), F.Identity, bias=160.0)
+        dma("y", [], [half("qout", l, 320)], T.qo[l:8:2, :], T.qout[0:128:32, 320 * l:320 * l + 320])
+    for sem, val in sorted(pending.items()):
+        g.wait_ge(T.sem[sem], val)
+    for sem, val in count.items():
+        g.wait_ge(T.sem[sem], val)

@@ -13,14 +13,14 @@ def _buf(dtype, **widths):
         SCRATCH[k] = ("sbuf", [128, n], dtype)
 
 
-_buf("bfloat16", xt=1280, xn0=1280, xn1=1280, xn2=1280, xp=1280, xi=1280, vt=1280, ht=1280, dp=1280, ut=512, vv=512, et=2048, ones=512,
-     iot=320, j16=320, df=320, ha=320, hb=320, hc=320, tw=64, qr=320, qmr=320, qir=320, mr=320, mqr=320, d0f=1280, d1f=1280, d0b=1280, d1b=1280,
-     tf=640, tb=640, w0=640, w1=640, zs=128, zt=192, sw=160, e1=128, e2=128, e3=128, e4=128, lf1=128, lf2=128, lb1=128, lb2=128,
-     sg0=320, sg1=320, frf=1600, frb=1600, tt=320, rr=160, rr8=160, mm=320, tm=320, ac=32, at=32, a2=32, bc=32, bt=32, md=32, cu0=64, cu1=64, cut=64)
-_buf("float32", ktm=40, ktn=40, ie=20, col=8, iwc=20, vf=10, qf=20, mf=20, qmw=20, qiw=20, mqw=20, wm=320, qout=640, yt=320)
-_buf("int32", icol=4, gqs=20, gms=20)
-_buf("uint16", offu=16, qo16=20, mo16=20, qio=20, kof=40, kob=40, lof=40, hif=40, tif=40, hib=40, tib=40, fl=20, sl=10, slb=10, ll=20, llb=20, xo=20, xob=20, moff=80, ktf=40, ktb=40)
-for _n, _w in (("uq", 128), ("us", 256), ("xq", 320), ("vq", 320), ("vvq", 128), ("eq", 512), ("wq", 512), ("hq", 960), ("rq", 960)):
+_buf("bfloat16", xt=1280, xn0=1280, xn1=1280, xn2=1280, xp=1280, xi=960, vt=1280, ht=1280, dp=1280, ut=512, vv=512, et=2048, ones=512,
+     iot=320, hs=80, hc=320, tw=48, z01=640, ys=640, yv=640, qr=320, qmr=320, qir=320, mr=320, mqr=320, d0f=640, d1f=640, d0b=640, d1b=640,
+     tf=320, tb=320, w=640, sg=320, frf=1440, frb=1440, t1=352, t1p=352, tt=320, rr=160, rr8=160, mm=320, tm=320,
+     ac=32, at=32, a2=32, bc=32, bt=32, md=32, cu0=32, cu1=32, cut=32)
+_buf("float32", sm=120, ie=20, col=16, iwc=20, vf=10, qf=20, mf=20, qmw=20, qiw=20, mqw=20, wm=320, qout=320, yt=320)
+_buf("int32", icol=4, offi=8, gqs=20, gms=20)
+_buf("uint16", offu=8, k16=20, qo16=20, mo16=20, qio=20, kof=20, kob=20, lof=20, hif=20, tif=20, hib=20, tib=20, fl=22, sl=10, slb=10, ll=20, llb=20, xo=20, xob=20, moff=32, ktf=20, ktb=20)
+for _n, _w in (("uq", 128), ("us", 128), ("xq", 320), ("vq", 320), ("vvq", 128), ("eq", 512), ("wq", 512), ("hq", 960), ("rq", 960)):
     SCRATCH[_n + "c"] = ("sbuf", [128, _w], "float8_e4m3fn_x4")
     SCRATCH[_n + "s"] = ("sbuf", [128, _w], "uint8")
 for _b in range(8):
@@ -29,9 +29,11 @@ for _b in range(8):
 NDMA = 20
 SEMAPHORES = ["qv", "qs", "qt", "qg", "lsem"] + ["d%d" % i for i in range(NDMA)] + ["ar%d_%d" % (r, h) for r in range(3) for h in range(2)]
 
-PLACE = {"kf": ("col", 0, 1), "mo": ("col", 1, 1), "me": ("col", 2, 1), "hh": ("col", 3, 1), "ca": ("col", 4, 1), "p31f": ("col", 5, 1),
-         "pi": ("icol", 0, 1), "ki": ("icol", 1, 1), "si": ("icol", 2, 1), "p31": ("icol", 3, 1),
-         "tw1": ("tw", 0, 16), "tw2": ("tw", 32, 32)}
+PLACE = {"tw1": ("tw", 0, 16), "tw2": ("tw", 32, 16)}
+PLACE.update({n: ("col", i, 1) for i, n in enumerate(("kf", "mo", "hh", "p31f", "s1", "b1", "s2", "b2", "gg", "sgo"))})
+PLACE.update({n: ("icol", i, 1) for i, n in enumerate(("pi", "ki", "si", "p31"))})
+PLACE.update({n: ("hs", 16 * i, 16) for i, n in enumerate(("j16", "df", "ha", "hb", "hc16"))})
+PLACE.update({n: ("sm", 20 * i, 20) for i, n in enumerate(("kw", "low", "hiw", "tiw", "kta", "ktc"))})
 
 
 def R(name, c0=0, c1=None, st=1, p0=0, p1=128):
@@ -39,10 +41,6 @@ def R(name, c0=0, c1=None, st=1, p0=0, p1=128):
         name, at, n = PLACE[name]
         return (name, at + c0, at + (n if c1 is None else c1), st, p0, p1)
     return (name, c0, SCRATCH[name][1][1] if c1 is None else c1, st, p0, p1)
-
-
-def half(name, l, n=640):
-    return R(name, n * l, n * l + n)
 
 
 def rank_program(g, core, T, topo):
@@ -64,7 +62,8 @@ def rank_program(g, core, T, topo):
     def hit(a, b):
         if a[4] >= b[5] or b[4] >= a[5] or a[1] >= b[2] or b[1] >= a[2]:
             return False
-        return not (a[3] == b[3] and a[3] > 1 and (a[1] - b[1]) % a[3])
+        s = min(a[3], b[3])
+        return not (s > 1 and max(a[3], b[3]) % s == 0 and (a[1] - b[1]) % s)
 
     def inside(a, b):
         return a[4] >= b[4] and a[5] <= b[5] and a[1] >= b[1] and a[2] <= b[2] and (b[3] == 1 or (a[3] == b[3] and (a[1] - b[1]) % a[3] == 0))
@@ -161,16 +160,15 @@ def rank_program(g, core, T, topo):
     def act(out, src, func, scale=1.0, bias=0.0):
         op("s", [out], [src], lambda: g.scalar.activation(ap(out), ap(src), func, bias=bias, scale=scale))
 
-    def wrap(src):
-        scan(R("wm"), R("hc"), src, A.add, A.max)
-        return R("wm", 15, 320, 16)
+    def unrow(dst, src):
+        scan(R("wm"), R("hc"), R(src), A.add, A.max)
+        ts(R(dst), R("wm", 15, 320, 16), one("hh"), A.subtract)
 
     waiting = []
 
-    def spare(n=1):
-        for _ in range(n):
-            if waiting:
-                waiting.pop(0)()
+    def spare():
+        if waiting:
+            waiting.pop(0)()
 
     dma("y", [R("gqs")], [], ap(R("gqs")), T.gq[:, :])
     dma("y", [R("gms")], [], ap(R("gms")), T.gm[:, :])
@@ -181,8 +179,8 @@ def rank_program(g, core, T, topo):
     dma("y", [R("wqs")], [], T.wqs[:, :], T.ws[:, :])
     dma("y", [R("vv")], [], ap(R("vv")), T.v[:, :])
 
-    def one(n):
-        return R(n, 0, 1)
+    def one(n, p0=0, p1=128):
+        return R(n, 0, 1, 1, p0, p1)
 
     def bits(out, s1, op0, s2=None, op1=None):
         if op1 is None:
@@ -191,17 +189,23 @@ def rank_program(g, core, T, topo):
             op("v", [one(out)], [one("pi")], lambda: g.vector.tensor_scalar(ap(one(out)), ap(one("pi")), s1, s2, op0, op1))
     op("g", [one("pi")], [], lambda: g.iota(ap(one("pi")), [[0, 1]], 0, 1))
     iota(R("ie"), [[16, 20]], 0, 0)
-    iota(R("j16"), [[0, 20], [1, 16]], 0, 0)
+    iota(R("j16"), [[1, 16]], 0, 0)
     iota(R("iot"), [[1, C]], -160, 0)
-    iota(R("d0f"), [[0, 1280]], 1024, 0)
+    op("g", [R("offi")], [], lambda: g.iota(ap(R("offi")), [[16, 8]], -16, 0))
+    iota(R("d0f"), [[0, 640]], 1024, 0)
+    for n in ("frf", "frb"):
+        iota(R(n, 0, 64), [[0, 64]], 0, 0)
+        iota(R(n, 704, 736), [[0, 32]], 0, 0)
+    iota(R("t1", 0, 16), [[0, 16]], 0, 0)
+    iota(R("t1", 336, 352), [[0, 16]], 0, 0)
+    iota(R("z01"), [[0, 320], [1, 2]], 0, 0)
+    iota(R("d0b"), [[0, 640]], 1024, 0)
+    iota(R("ac"), [[0, 32]], 0, 0)
+    iota(R("bc"), [[0, 32]], 0, 0)
     iota(R("ones"), [[0, 512]], 1, 0)
     for b in range(4):
         o = R("et", 512 * b, 512 * b + 512)
         op("g", [o], [R("ones")], lambda o=o, b=b: g.affine_select(ap(o), ap(R("ones")), [[-1, 512]], A.is_equal, 0.0, b, 4))
-    iota(R("d0b"), [[0, 1280]], 1024, 0)
-    for e in range(8):
-        q, l = e % 4, e // 4
-        fill(R("offu", 2 * e, 2 * e + 2), 16 * ((2 * q + l + 7) % 8))
     bits("ki", 15, A.bitwise_and)
     bits("si", 4, A.arith_shift_right, 1, A.bitwise_and)
     bits("p31", 31, A.bitwise_and)
@@ -209,13 +213,18 @@ def rank_program(g, core, T, topo):
     copy(one("mo"), one("si"))
     copy(one("p31f"), one("p31"))
     ts(one("hh"), one("kf"), 15.0, A.is_lt, 512.0, A.mult)
-    ts(one("me"), one("mo"), -1.0, A.mult, 1.0, A.add)
     ts(R("df"), R("j16"), one("kf"), A.subtract)
-    ts(one("ca"), one("hh"), 160.5, A.subtract)
+    ts(R("k16"), R("ie"), 0.0, A.mult, one("kf"), A.add)
     ts(R("ha"), R("df"), 0.0, A.is_equal, -4096.0, A.mult)
     ts(R("hb"), R("df"), 1.0, A.is_equal, 512.0, A.mult)
     ts(R("iwc"), R("ie"), one("kf"), A.add, 160.0, A.subtract)
-    fill(R("zs"), 0.0)
+    tt(R("hc16"), R("ha"), R("hb"), A.add)
+    pick("s", R("hc"), R("hc16"), R("k16"))
+    for n, c, v in (("tw1", 0, -512.0), ("tw2", 0, 512.0)):
+        fill(R(n, 0, 1), v)
+        fill(R(n, 1, 16), -v)
+    for n, a, b in (("s1", -1.0, 2.0), ("b1", 511.0, 385.0), ("s2", 1.0, 1.0), ("b2", -543.0, 928.0), ("gg", -16.0, 1264.0), ("sgo", -16.0, 176.0)):
+        ts(one(n), one("mo"), a, A.mult, b, A.add)
 
     copy(R("qo16"), R("gqs"))
     copy(R("mo16"), R("gms"))
@@ -223,88 +232,79 @@ def rank_program(g, core, T, topo):
     ts(R("qf"), R("gqs"), 160.0, A.subtract)
     ts(R("mf"), R("gms"), 160.0, A.subtract)
     pick("v", R("qmr"), R("qr"), R("mo16"))
-    tt(R("zs", 0, 20), R("iwc"), R("mf"), A.min)
-    tt(R("hc"), R("ha"), R("hb"), A.add)
-    fill(R("tw1", 0, 1), -512.0)
-    w = wrap(R("qmr"))
+    tt(R("kw"), R("iwc"), R("mf"), A.min)
+    copy(R("offu"), R("offi"))
+    unrow("qmw", "qmr")
+    fill(R("offu", 0, 1), 112)
     quant("uq", R("ut"), 0, 128)
-    ts(R("qmw"), w, one("hh"), A.subtract)
-    op("s", [R("uss")], [R("uqs"), R("offu")], lambda: g.scalar.activation(T.uss[:, 0:256], T.uqs[:, 0:128].indirect(T.offu[:, 0:16]), F.Copy))
+    ts(R("kof"), R("kw"), 160.0, A.add)
+    op("s", [R("uss")], [R("uqs"), R("offu")], lambda: g.scalar.activation(T.uss[:, 0:128], T.uqs[:, 0:128].indirect(T.offu[:, 0:8]), F.Copy))
+
+    def tables(d, qw, qmw):
+        tt(R("tiw"), R(qmw), R(qw), A.is_gt)
+        tt(R("hiw"), R(qw), R(qmw), A.max)
+        tt(R("low"), R(qw), R(qmw), A.min)
+        copy(R("ti" + d), R("tiw"))
+        ts(R("hi" + d), R("hiw"), 160.0, A.add)
+        ts(R("lof" if d == "f" else "kob"), R("low"), 160.0, A.add)
+        pick("s", R("t" + d), R("tw1"), R("ti" + d))
+        pick("v" if d == "f" else "s", R("d1" + d, 1, 640, 2), R("iot"), R("hi" + d))
+        pick("s", R("d0" + d, 1, 640, 2), R("iot"), R("lof" if d == "f" else "kob"))
+
+    def window_list(d, kw):
+        ts(R("kta"), R("tiw"), -320.0, A.mult, 480.0, A.add)
+        tt(R("ktc"), R("kta"), R(kw), A.add)
+        copy(R("kt" + d), R("ktc"))
+
+    def signs(moving, h):
+        c0, c1 = HALVES[h]
+        mx(h, c1 - c0, "us", 0, moving, c0)
+        act(R("sg", c0, c1), R("ps%d" % h, 0, c1 - c0), F.Sign, bias=-EPS)
+
+    def halves(name, src, decide):
+        for h, (c0, c1) in enumerate(HALVES):
+            quant(name, R(src, 4 * c0, 4 * c1), c0, c1)
+            if decide:
+                signs(name, h)
+
+    op("v", [R("usc")], [R("uqc"), R("offu")], lambda: g.vector.tensor_copy(T.usc[:, 0:128].bitcast(dt.uint32), T.uqc[:, 0:128].bitcast(dt.uint32).indirect(T.offu[:, 0:8])))
+    tables("f", "qf", "qmw")
+    halves("xq", "xt", True)
     pick("s", R("mr"), R("iot"), R("mo16"))
-    fill(R("zt"), 0.0)
-    tt(R("zs", 32, 52), R("qf"), R("qmw"), A.min)
-    tt(R("zs", 64, 84), R("qf"), R("qmw"), A.max)
-    tt(R("zs", 96, 116), R("qmw"), R("qf"), A.is_gt)
-    fill(R("tw1", 1, 16), 512.0)
-
-    def spread(o1, o2):
-        return [lambda: turn(R("zt", 32, 160), R("zs")),
-                lambda: ts(R("e1"), R("zs"), one("me"), A.mult),
-                lambda: ts(R("e3"), R("zs"), one("mo"), A.mult),
-                lambda: turn(R("sw"), R("zt", 16, 176)),
-                lambda: ts(R("e2"), R("sw", 0, 128), one("mo"), A.mult),
-                lambda: ts(R("e4"), R("sw", 32, 160), one("me"), A.mult),
-                lambda: tt(R(o1), R("e1"), R("e2"), A.add),
-                lambda: tt(R(o2), R("e3"), R("e4"), A.add)]
-
-    def offs(name, l, slot, add):
-        ts(half(name, l, 20), R("l%s%d" % (name[2], l + 1), 32 * slot, 32 * slot + 20), add, A.add)
-
-    for f in spread("lf1", "lf2"):
-        f()
-    offs("tif", 0, 3, 0.0)
-    offs("hif", 0, 2, 160.0)
-    pick("s", half("tf", 0, 320), R("tw1"), half("tif", 0, 20))
-    op("v", [R("usc")], [R("uqc"), R("offu")], lambda: g.vector.tensor_copy(T.usc[:, 0:256].bitcast(dt.uint32), T.uqc[:, 0:128].bitcast(dt.uint32).indirect(T.offu[:, 0:16])))
-    quant("xq", R("xt"), 0, C)
-    offs("kof", 0, 0, 160.0)
-    offs("lof", 0, 1, 160.0)
-    pick("s", R("d0f", 1, 640, 2), R("iot"), half("lof", 0, 20))
-
-    def signs(l, moving):
-        mx(l, C, "us", 128 * l, moving, 0)
-        act(R("sg%d" % l), R("ps%d" % l, 0, C), F.Sign, bias=-EPS)
 
     def ring():
         state["bank"] += 1
         return 2 + state["bank"] % 6
 
-    signs(0, "xq")
-    signs(1, "xq")
-    pick("v", R("d1f", 1, 640, 2), R("iot"), half("hif", 0, 20))
-    for n, slot, add in (("tif", 3, 0.0), ("hif", 2, 160.0), ("kof", 0, 160.0), ("lof", 1, 160.0)):
-        offs(n, 1, slot, add)
-    pick("s", half("tf", 1, 320), R("tw1"), half("tif", 1, 20))
-    pick("s", R("d1f", 641, 1280, 2), R("iot"), half("hif", 1, 20))
-    pick("s", R("d0f", 641, 1280, 2), R("iot"), half("lof", 1, 20))
+    def choose(d):
+        pick_tt(R("d1" + d, 0, 640, 2), R("sg"), R("ko" + d), R("t" + d), A.mult)
 
-    def choose(d, l):
-        pick_tt(R("d1" + d, 640 * l, 640 * l + 640, 2), R("sg%d" % l), half("ko" + d, l, 20), half("t" + d, l, 320), A.mult)
+    def rows(d):
+        scan(R("fr" + d, 64, 704), R("d0" + d), R("d1" + d), A.max, A.min)
 
-    def rows(d, l):
-        scan(half("fr" + d, l), half("d0" + d, l), half("d1" + d, l), A.max, A.min)
-
-    def lists(d, q, src, st, with_sl):
-        s = R("tt", 0, 10 * st, st, 32 * src, 32 * src + 32)
-        sl, ll = ("sl", "ll") if d == "f" else ("slb", "llb")
-        p = (32 * q, 32 * q + 32)
-        if with_sl == 1:
-            ts(R(sl, 0, 10, 1, *p), s, 160.0, A.add)
-        if d == "f":
-            ts(R(ll, 0, 20, 2, *p), s, 160.5, A.add, 2.0, A.mult)
-            ts(R(ll, 1, 20, 2, *p), s, 1440.0, A.add)
+    def place(kind, out, s, p0=0, p1=128):
+        if kind in "12":
+            ts(out, s, one("s" + kind, p0, p1), A.mult, one("b" + kind, p0, p1), A.add)
         else:
-            ts(R(ll, 0, 20, 2, *p), s, 1440.0, A.add)
-            ts(R(ll, 1, 20, 2, *p), s, 480.5, A.add, 2.0, A.mult)
-        if with_sl == 2:
-            ts(R(sl, 0, 10, 1, *p), s, 160.0, A.add)
+            ts(out, s, one(kind, p0, p1), A.add)
+
+    def lists(d, q, s, p0, p1, with_sl):
+        sl, ll = ("sl", "ll") if d == "f" else ("slb", "llb")
+        p = (32 * q, 32 * q + p1 - p0)
+        todo = [lambda: place("1" if d == "f" else "gg", R(ll, 0, 20, 2, *p), s, p0, p1), lambda: place("gg" if d == "f" else "2", R(ll, 1, 20, 2, *p), s, p0, p1)]
+        one_more = lambda: place("sgo", R(sl, 0, 10, 1, *p), s, p0, p1)
+        for f in ([one_more] if with_sl == 1 else []) + todo + ([one_more] if with_sl == 2 else []):
+            f()
+
+    def turned(q, st):
+        return R("tt", 0, 10 * st, st, 32 * q, 32 * q + 32), 32 * q, 32 * q + 32
 
     def step(d, q, to, with_sl):
-        pick("v", R("rr"), R("fr" + d, 1280, 1600), R("sl" if d == "f" else "slb"))
+        pick("v", R("rr"), R("fr" + d, 1088, 1440), R("sl" if d == "f" else "slb"))
         spare()
         turn(R("tt", 0, 160, 1, 32 * q, 32 * q + 32), R("rr", 0, 160, 1, 32 * q, 32 * q + 32))
         spare()
-        lists(d, to, q, 16, with_sl)
+        lists(d, to, *turned(q, 16), with_sl)
 
     def finish(d, out, crossed):
         pick("v", R("mm"), R("fr" + d), R("ll" if d == "f" else "llb"))
@@ -318,99 +318,89 @@ def rank_program(g, core, T, topo):
             ts(R(out, 1, 20, 4, *p), R("tm", 32, 320, 64, *p), 160.0, A.add)
             ts(R(out, 2, 20, 4, *p), R("tm", 16, 320, 64, *p), 160.0, A.add)
 
-    def compose(d, first):
-        w = wrap(R("fr" + d, 640 * first + 1, 640 * first + 640, 2))
-        rows(d, 1 - first)
-        ts(R("fl"), w, one("ca"), A.subtract, 2.0, A.mult)
+    def compose(d, between):
+        fr, o = "fr" + d, 0 if d == "f" else 16
+        turn(R("t1", 16, 336), R(fr, 65, 704, 2))
+        turn(R("t1p"), R(fr, 33, 736, 2))
+        turn(R(fr, 736, 1088), R("t1"))
+        k = "2" if d == "f" else "1"
+        place(k, R("fl", 0, 22, 2), R("t1p", o, 352, 32))
+        place(k, R("fl", 1, 20, 2), R("t1", 16 + o, 336, 32))
+        between()
+        pick("v", R(fr, 1088, 1440), R(fr, 0, 1088), R("fl"))
         spare()
-        pick("v", R("fr" + d, 1280, 1600), half("fr" + d, 1 - first), R("fl"))
 
     def planes(src):
         for t in range(4):
             act(R("xp", C * t, C * t + C), R(src, t, 1280, 4), F.Copy, scale=0.5)
-        act(R("xi"), R(src), F.Copy, scale=0.5)
+            act(R("xi", C * t, C * t + C) if t < 3 else R("ys", 0, 640, 2), R(src, t, 1280, 4), F.Copy, scale=0.5)
 
-    planes("xt")
+    def passes(out, win, off, other, pairs, between):
+        def fused(t):
+            pick_tt(R(out, t, 1280, 4), R(win, C * t, C * t + C), R(off), other(t), A.add)
+        pick("s", R(pairs, 1, 640, 2), R(win, 960, 1280), R(off))
+        fused(0)
+        between[0]()
+        scan(R(out, 1, 1280, 2), R("z01"), R(pairs), A.mult, A.add)
+        between[1]()
+        fused(2)
+        fused(1)
+
     ts(R("vf"), R("ie", 0, 10), 2.0, A.mult, one("p31f"), A.add)
+    fill(R("fl", 20, 22), 0)
+    ts(R("vf"), R("vf"), 160.0, A.subtract)
+    lists("f", 0, R("vf"), 0, 128, 1)
+    window_list("f", "kw")
     waiting += [
         lambda: op("v", [R("qir")], [R("qo16"), R("iot")], lambda: g.vector.tensor_copy(ap(R("qir")).indirect(ap(R("qo16"))), ap(R("iot")))),
-        lambda: ts(R("qiw"), wrap(R("qir")), one("hh"), A.subtract),
+        lambda: unrow("qiw", "qir"),
         lambda: ts(R("qio"), R("qiw"), 160.0, A.add),
-        lambda: pick("s", R("mqr"), R("mr"), R("qio")),
-        lambda: ts(R("mqw"), wrap(R("mqr")), one("hh"), A.subtract),
-        lambda: (tt(R("zs", 32, 52), R("qiw"), R("mqw"), A.min), tt(R("zs", 64, 84), R("qiw"), R("mqw"), A.max), tt(R("zs", 96, 116), R("mqw"), R("qiw"), A.is_gt))]
-    waiting += spread("lb1", "lb2")
+        lambda: (pick("s", R("mqr"), R("mr"), R("qio")), planes("xt")),
+        lambda: lists("b", 0, R("vf"), 0, 128, 1),
+        lambda: copy(R("ac", 0, 20), R("iwc")),
+        lambda: unrow("mqw", "mqr"),
+        lambda: turn(R("at"), R("ac")),
+        lambda: tables("b", "qiw", "mqw"),
+        lambda: copy(R("a2", 0, 16, 1, 0, 32), R("at", 0, 16, 1, 0, 32)),
+        lambda: window_list("b", "low")]
 
-    def back_offs(l):
-        for n, slot, add in (("tib", 3, 0.0), ("hib", 2, 160.0), ("kob", 1, 160.0)):
-            offs(n, l, slot, add)
-        pick("s", half("tb", l, 320), R("tw1"), half("tib", l, 20))
-        pick("s", R("d1b", 640 * l + 1, 640 * l + 640, 2), R("iot"), half("hib", l, 20))
-        pick("s", R("d0b", 640 * l + 1, 640 * l + 640, 2), R("iot"), half("kob", l, 20))
-    waiting += [lambda: back_offs(1), lambda: back_offs(0)]
-    copy(R("sl"), R("vf"))
-    ts(R("ll", 0, 20, 2), R("vf"), 2.0, A.mult, 1.0, A.add)
-    ts(R("ll", 1, 20, 2), R("vf"), 1280.0, A.add)
-
-    def leftover():
-        copy(R("slb"), R("vf"))
-        ts(R("llb", 0, 20, 2), R("vf"), 1280.0, A.add)
-        ts(R("llb", 1, 20, 2), R("vf"), 2.0, A.mult, 641.0, A.add)
-        for n in ("ac", "bc"):
-            fill(R(n), 0.0)
-        for c0, c1, v in ((0, 1, 512.0), (1, 16, -512.0), (16, 17, -512.0), (17, 32, 512.0)):
-            fill(R("tw2", c0, c1), v)
-        copy(R("ac", 0, 20), R("iwc"))
-        quant("eq", R("et"), 0, 512)
-        turn(R("at"), R("ac"))
-        quant("vvq", R("vv"), 0, 128)
-        copy(R("a2", 0, 16, 1, 0, 32), R("at", 0, 16, 1, 0, 32))
-
-    def window_lists():
-        res = []
-        for d, slot in (("f", 0), ("b", 1)):
-            res += [lambda d=d, l=l: ts(half("ktm", l, 20), R("l%s%d" % (d, l + 1), 96, 116), -320.0, A.mult, 480.0, A.add) for l in range(2)]
-            res += [lambda d=d, l=l, slot=slot: tt(half("ktn", l, 20), half("ktm", l, 20), R("l%s%d" % (d, l + 1), 32 * slot, 32 * slot + 20), A.add) for l in range(2)]
-            res += [lambda d=d: copy(R("kt" + d), R("ktn"))]
-        return res
+    def nothing():
+        pass
 
     for rnd, s in enumerate(ROUNDS):
         peer = T.cores[rank ^ s]
         rid, pid, _se = topo.addr(peer)
         mask, neng = topo.mask(core, peer), len(topo.engines(core, peer))
-        choose("f", 0)
-        choose("f", 1)
-        rows("f", 0)
-        compose("f", 0)
+        choose("f")
         spare()
-        turn(R("tt", 0, 320, 1, 0, 32), R("frf", 1280, 1600, 1, 0, 32))
+        rows("f")
         spare()
-        lists("f", 1, 0, 32, 1)
+        compose("f", spare)
+        turn(R("tt", 0, 320, 1, 0, 32), R("frf", 1104, 1424, 1, 0, 32))
+        spare()
+        lists("f", 1, *turned(0, 32), 1)
         step("f", 1, 2, 1)
         step("f", 2, 3, 2)
         finish("f", "xo", (2,))
         while waiting:
             spare()
-        for t in range(4):
-            pick_tt(R("vt", t, 1280, 4), R("xp", C * t, C * t + C), R("xo"), R("xi", t, 1280, 4), A.add)
-        quant("vq", R("vt"), 0, C)
-        signs(1, "vq")
-        signs(0, "vq")
+        passes("vt", "xp", "xo", lambda t: R("xi", C * t, C * t + C), "ys", (nothing, nothing))
+        halves("vq", "vt", True)
         for h, (c0, c1) in enumerate(HALVES):
             for b in range(4):
                 k = ring()
                 mx(k, c1 - c0, "wq", 128 * b, "vq", c0)
                 act(R("ht", 4 * c0 + b, 4 * c1, 4), R("ps%d" % k, 0, c1 - c0), F.Copy, scale=0.03125)
-        if rnd == 0:
-            leftover()
-        pick("v", R("rr8"), R("frf", 1280, 1600), R("sl"))
+        act(R("yv", 0, 640, 2), R("vt", 3, 1280, 4), F.Copy)
+        pick("v", R("rr8"), R("frf", 1088, 1440), R("sl"))
         ts(R("ac", 0, 20), R("xo"), 160.0, A.subtract)
         turn(R("tt", 0, 160, 1, 96, 128), R("rr8", 0, 160, 1, 96, 128))
         turn(R("at"), R("ac"))
-        lists("b", 3, 3, 16, 1)
-        copy(R("a2", 16, 32), R("at", 0, 16))
-        for q in range(3):
-            copy(R("a2", 0, 16, 1, 32 * q + 32, 32 * q + 64), R("at", 16, 32, 1, 32 * q, 32 * q + 32))
+        lists("b", 3, *turned(3, 16), 1)
+        if rnd == 0:
+            quant("vvq", R("vv"), 0, 128)
+        waiting.append(lambda: copy(R("a2", 16, 32), R("at", 0, 16)))
+        waiting += [lambda q=q: copy(R("a2", 0, 16, 1, 32 * q + 32, 32 * q + 64), R("at", 16, 32, 1, 32 * q, 32 * q + 32)) for q in range(3)]
 
         def send(h):
             c0, c1 = C * rnd + HALVES[h][0], C * rnd + HALVES[h][1]
@@ -424,17 +414,15 @@ def rank_program(g, core, T, topo):
             clock[(sem, 2 * neng)] = {}
             note([R("rqc", c0, c1), R("rqs", c0, c1)], [], (sem, 2 * neng))
 
-        choose("b", 1)
-        choose("b", 0)
-        send(0)
-        rows("b", 1)
-        send(1)
-        if rnd == 0:
-            waiting += window_lists()
-        compose("b", 1)
+        choose("b")
         spare()
+        rows("b")
+        send(0)
+        compose("b", lambda: send(1))
         step("b", 3, 2, 1)
         step("b", 2, 1, 1)
+        if rnd == 0:
+            quant("eq", R("et"), 0, 512)
         step("b", 1, 0, 0)
         for h, (c0, c1) in enumerate(HALVES):
             for b in range(4):
@@ -445,53 +433,36 @@ def rank_program(g, core, T, topo):
         while waiting:
             spare()
         xn = "xn%d" % rnd
+        last = rnd == 2
 
-        def part(t):
-            pick_tt(R(xn, t, 1280, 4), R("dp", C * t, C * t + C), R("xob"), R("vt", t, 1280, 4), A.add)
-
-        def tables(d, l):
-            pick("s", half("t" + d, l, 320) if rnd < 2 else R("d1f", 640 * l, 640 * l + 640, 2), R("w%d" % l), half("kt" + d, l, 20))
+        def misses():
+            cu, old = "cu%d" % (rnd % 2), "cu%d" % (1 - rnd % 2)
+            tt(R("md" if rnd else cu), R("a2"), R("bt"), A.not_equal)
+            if rnd:
+                tt(R(cu), R(old), R("md"), A.not_equal)
+            turn(R("cut"), R(cu))
+            copy(R("moff"), R("cut"))
+            a, b = (320, 0) if last else (0, 320)
+            pick("s", R("w", a, a + 320), R("tw2"), R("moff", 0, 20))
+            act(R("w", b, b + 320), R("w", a, a + 320), F.Copy, scale=-1.0)
+            pick("s", R("d1f", 0, 640, 2) if last else R("tf"), R("w"), R("ktf"))
         ts(R("bc", 0, 20), R("xob"), 160.0, A.subtract)
-        part(0)
-        turn(R("bt"), R("bc"))
-        cu, old = "cu%d" % (rnd % 2), "cu%d" % (1 - rnd % 2)
-        pairs = ((16, 48, 0, 32), (0, 16, 0, 16), (48, 64, 16, 32))
-        if rnd == 0:
-            for c0, c1, m0, m1 in pairs:
-                tt(R(cu, c0, c1), R("a2", m0, m1), R("bt", m0, m1), A.not_equal)
-        else:
-            tt(R("md"), R("a2"), R("bt"), A.not_equal)
-            for c0, c1, m0, m1 in pairs:
-                tt(R(cu, c0, c1), R(old, 16 + m0, 16 + m1), R("md", m0, m1), A.not_equal)
-        turn(R("cut"), R(cu))
-        for l in range(2):
-            for k in range(2):
-                ts(R("moff", 40 * l + 20 * k, 40 * l + 20 * k + 20), R("cut", 32 * l, 32 * l + 20), 16.0 * (k if rnd < 2 else 1 - k), A.add)
-        pick("s", R("w0"), R("tw2"), half("moff", 0, 40))
-        tables("f", 0)
-        pick("s", R("w1"), R("tw2"), half("moff", 1, 40))
-        for t in (1, 2, 3):
-            part(t)
-        quant("xq", R(xn), 0, C)
-        if rnd < 2:
-            signs(0, "xq")
-            tables("f", 1)
-            signs(1, "xq")
+        passes(xn, "dp", "xob", lambda t: R("vt", t, 1280, 4), "yv", (lambda: turn(R("bt"), R("bc")), misses))
+        halves("xq", xn, not last)
+        if not last:
             planes(xn)
-            tables("b", 1)
-            tables("b", 0)
+            pick("s", R("tb"), R("w"), R("ktb"))
 
-    mx(0, C, "vvq", 0, "xq", 0)
+    for h, (c0, c1) in enumerate(HALVES):
+        mx(h, c1 - c0, "vvq", 0, "xq", c0)
+        copy(R("yt", c0, c1), R("ps%d" % h, 0, c1 - c0))
+        dma("y", [], [R("yt", c0, c1)], T.y[:, c0:c1], ap(R("yt", c0, c1)))
+    rows("f")
+    act(R("qout"), R("frf", 65, 704, 2), F.Identity, bias=160.0)
+    dma("s", [], [R("qout")], T.qo[:, :], T.qout[0:128:16, :])
     dma("y", [], [R("xqc")], T.oc[:, :], T.xqc[:, :].bitcast(dt.uint8))
     for k in range(4):
         dma("y", [], [R("xqs")], T.osc[4 * k:4 * k + 4, :], T.xqs[32 * k:32 * k + 4, :])
-    act(R("yt"), R("ps0", 0, C), F.Copy)
-    dma("s", [], [R("yt")], T.y[:, :], ap(R("yt")))
-    tables("f", 1)
-    for l in range(2):
-        rows("f", l)
-        act(half("qout", l, 320), R("frf", 640 * l + 1, 640 * l + 640, 2), F.Identity, bias=160.0)
-        dma("y", [], [half("qout", l, 320)], T.qo[l:8:2, :], T.qout[0:128:32, 320 * l:320 * l + 320])
     for sem, val in sorted(pending.items()):
         g.wait_ge(T.sem[sem], val)
     for sem, val in count.items():

from concourse.mybir import dt, AluOpType as A, ActivationFunctionType as F

C = 320
ROUNDS = (1, 2, 4)
HALVES = ((0, 160), (160, 320))
EPS = 2.0 ** -93

SCRATCH = {}


def _buf(dtype, **widths):
    for k, n in widths.items():
        SCRATCH[k] = ("sbuf", [128, n], dtype)


_buf("bfloat16", xt=1280, xn0=1280, xn1=1280, xn2=1280, xp=1280, xi=960, vt=1280, ht=1280, dp=1280, ut=512, vv=512, et=2048, ones=512,
     iot=320, hs=80, hc=320, tw=48, z01=640, ys=640, yv=640, qr=320, qmr=320, qir=320, mr=320, mqr=320, d0f=640, d1f=640, d0b=640, d1b=640,
     tf=320, tb=320, w=640, sg=320, frf=1440, frb=1440, t1=352, t1p=352, tt=320, rr=160, rr8=160, mm=320, tm=320,
     ac=32, at=32, a2=32, bc=32, bt=32, md=32, cu0=32, cu1=32, cut=32)
_buf("float32", sm=120, ie=20, col=16, iwc=20, vf=10, qf=20, mf=20, qmw=20, qiw=20, mqw=20, wm=320, qout=320, yt=320)
_buf("int32", icol=4, offi=8, gqs=20, gms=20)
_buf("uint16", offu=8, k16=20, qo16=20, mo16=20, qio=20, kof=20, kob=20, lof=20, hif=20, tif=20, hib=20, tib=20, fl=22, sl=10, slb=10, ll=20, llb=20, xo=20, xob=20, moff=32, ktf=20, ktb=20)
for _n, _w in (("uq", 128), ("us", 128), ("xq", 320), ("vq", 320), ("vvq", 128), ("eq", 512), ("wq", 512), ("hq", 960), ("rq", 960)):
    SCRATCH[_n + "c"] = ("sbuf", [128, _w], "float8_e4m3fn_x4")
    SCRATCH[_n + "s"] = ("sbuf", [128, _w], "uint8")
for _b in range(8):
    SCRATCH["ps%d" % _b] = ("psum", [128, 512], "float32")

NDMA = 20
SEMAPHORES = ["qv", "qs", "qt", "qg", "lsem"] + ["d%d" % i for i in range(NDMA)] + ["ar%d_%d" % (r, h) for r in range(3) for h in range(2)]

PLACE = {"tw1": ("tw", 0, 16), "tw2": ("tw", 32, 16)}
PLACE.update({n: ("col", i, 1) for i, n in enumerate(("kf", "mo", "hh", "p31f", "s1", "b1", "s2", "b2", "gg", "sgo"))})
PLACE.update({n: ("icol", i, 1) for i, n in enumerate(("pi", "ki", "si", "p31"))})
PLACE.update({n: ("hs", 16 * i, 16) for i, n in enumerate(("j16", "df", "ha", "hb", "hc16"))})
PLACE.update({n: ("sm", 20 * i, 20) for i, n in enumerate(("kw", "low", "hiw", "tiw", "kta", "ktc"))})


def R(name, c0=0, c1=None, st=1, p0=0, p1=128):
    if name in PLACE:
        name, at, n = PLACE[name]
        return (name, at + c0, at + (n if c1 is None else c1), st, p0, p1)
    return (name, c0, SCRATCH[name][1][1] if c1 is None else c1, st, p0, p1)


def rank_program(g, core, T, topo):
    rank = T.rank_of(core)
    if rank is None:
        return
    queue = {"v": g.vector, "s": g.scalar, "t": g.tensor, "g": g, "y": g.sync}
    count = {"qv": 0, "qs": 0, "qt": 0, "qg": 0}
    known = {k: {} for k in queue}
    clock = {}
    writes, reads = {}, {}
    pending = {}
    state = {"bank": 0, "dma": 0}

    def ap(r):
        name, c0, c1, st, p0, p1 = r
        return T[name][p0:p1, c0:c1:st] if st > 1 else T[name][p0:p1, c0:c1]

    def hit(a, b):
        if a[4] >= b[5] or b[4] >= a[5] or a[1] >= b[2] or b[1] >= a[2]:
            return False
        s = min(a[3], b[3])
        return not (s > 1 and max(a[3], b[3]) % s == 0 and (a[1] - b[1]) % s)

    def inside(a, b):
        return a[4] >= b[4] and a[5] <= b[5] and a[1] >= b[1] and a[2] <= b[2] and (b[3] == 1 or (a[3] == b[3] and (a[1] - b[1]) % a[3] == 0))

    def settle(q, events):
        for sem, val in sorted(events, key=lambda e: (-len(clock[e]), e[0], -e[1])):
            if known[q].get(sem, 0) < val:
                queue[q].wait_ge(T.sem[sem], val)
                for s, v in clock[(sem, val)].items():
                    known[q][s] = max(known[q].get(s, 0), v)
                known[q][sem] = val

    def order(q, outs, ins):
        ev = set()
        for r in ins:
            ev |= {e for w, e in writes.get(r[0], []) if hit(r, w)}
        for r in outs:
            ev |= {e for w, e in writes.get(r[0], []) if hit(r, w)}
            ev |= {e for w, e in reads.get(r[0], []) if hit(r, w) and e[0] != "q" + q}
        settle(q, ev)

    def note(outs, ins, ev):
        for r in outs:
            for book in (writes, reads):
                book[r[0]] = [(w, e) for w, e in book.get(r[0], []) if not inside(w, r)]
            writes[r[0]].append((r, ev))
        for r in ins:
            reads.setdefault(r[0], []).append((r, ev))

    def op(q, outs, ins, fn):
        order(q, outs, ins)
        sem = "q" + q
        clk = dict(known[q])
        fn().then_inc(T.sem[sem], 1)
        count[sem] += 1
        clk[sem] = count[sem]
        clock[(sem, count[sem])] = clk
        note(outs, ins, (sem, count[sem]))

    def dma(q, outs, ins, dst, src):
        order(q, outs, ins)
        sem = "d%d" % state["dma"]
        state["dma"] += 1
        clock[(sem, 16)] = dict(known[q])
        queue[q].dma_start(dst, src).then_inc(T.sem[sem], 16)
        pending[sem] = 16
        note(outs, ins, (sem, 16))

    def copy(out, src):
        op("v", [out], [src], lambda: g.vector.tensor_copy(ap(out), ap(src)))

    def pick(q, out, win, off):
        if q == "v":
            op(q, [out], [win, off], lambda: g.vector.tensor_copy(ap(out), ap(win).indirect(ap(off))))
        else:
            op(q, [out], [win, off], lambda: g.scalar.activation(ap(out), ap(win).indirect(ap(off)), F.Copy))

    def pick_tt(out, win, off, other, alu):
        op("v", [out], [win, off, other], lambda: g.vector.tensor_tensor(ap(out), ap(win).indirect(ap(off)), ap(other), alu))

    def ts(out, src, s1, op0, s2=None, op1=None):
        col = [s for s in (s1, s2) if isinstance(s, tuple)]
        a1 = ap(s1) if isinstance(s1, tuple) else s1
        a2 = ap(s2) if isinstance(s2, tuple) else s2
        if op1 is None:
            op("v", [out], [src] + col, lambda: g.vector.tensor_scalar(ap(out), ap(src), a1, None, op0))
        else:
            op("v", [out], [src] + col, lambda: g.vector.tensor_scalar(ap(out), ap(src), a1, a2, op0, op1))

    def tt(out, a, b, alu):
        op("v", [out], [a, b], lambda: g.vector.tensor_tensor(ap(out), ap(a), ap(b), alu))

    def fill(out, val):
        op("v", [out], [], lambda: g.vector.memset(ap(out), val))

    def iota(out, pattern, base, cm):
        op("g", [out], [], lambda: g.iota(ap(out), pattern, base, cm, allow_small_or_imprecise_dtypes=True))

    def turn(out, src):
        op("v", [out], [src], lambda: g.vector.transpose(ap(out), ap(src)))

    def scan(out, d0, d1, op0, op1):
        op("v", [out], [d0, d1], lambda: g.vector.tensor_tensor_scan(ap(out), ap(d0), ap(d1), 0.0, op0, op1))

    def quant(name, src, c0, c1):
        o, s = R(name + "c", c0, c1), R(name + "s", c0, c1)
        op("v", [o, s], [src], lambda: g.vector.quantize_mx(ap(o), ap(s), ap(src)))

    def mx(bank, n, wname, w0, mname, m0):
        w, ws, m, ms = R(wname + "c", w0, w0 + 128), R(wname + "s", w0, w0 + 128), R(mname + "c", m0, m0 + n), R(mname + "s", m0, m0 + n)
        o = R("ps%d" % bank, 0, n)
        op("t", [R("ps%d" % bank)], [w, ws, m, ms], lambda: g.tensor.matmul_mx(ap(o), ap(w), ap(ws), ap(m), ap(ms), True, True))

    def act(out, src, func, scale=1.0, bias=0.0):
        op("s", [out], [src], lambda: g.scalar.activation(ap(out), ap(src), func, bias=bias, scale=scale))

    def unrow(dst, src):
        scan(R("wm"), R("hc"), R(src), A.add, A.max)
        ts(R(dst), R("wm", 15, 320, 16), one("hh"), A.subtract)

    waiting = []

    def spare():
        if waiting:
            waiting.pop(0)()

    dma("y", [R("gqs")], [], ap(R("gqs")), T.gq[:, :])
    dma("y", [R("gms")], [], ap(R("gms")), T.gm[:, :])
    dma("y", [R("xt")], [], ap(R("xt")), T.x[:, :])
    dma("s", [R("ut")], [], ap(R("ut")), T.u[:, :])
    order("y", [], [R("xt")])
    dma("y", [R("wqc")], [], T.wqc[:, :].bitcast(dt.uint8), T.wc[:, :])
    dma("y", [R("wqs")], [], T.wqs[:, :], T.ws[:, :])
    dma("y", [R("vv")], [], ap(R("vv")), T.v[:, :])

    def one(n, p0=0, p1=128):
        return R(n, 0, 1, 1, p0, p1)

    def bits(out, s1, op0, s2=None, op1=None):
        if op1 is None:
            op("v", [one(out)], [one("pi")], lambda: g.vector.tensor_scalar(ap(one(out)), ap(one("pi")), s1, None, op0))
        else:
            op("v", [one(out)], [one("pi")], lambda: g.vector.tensor_scalar(ap(one(out)), ap(one("pi")), s1, s2, op0, op1))
    op("g", [one("pi")], [], lambda: g.iota(ap(one("pi")), [[0, 1]], 0, 1))
    iota(R("ie"), [[16, 20]], 0, 0)
    iota(R("j16"), [[1, 16]], 0, 0)
    iota(R("iot"), [[1, C]], -160, 0)
    op("g", [R("offi")], [], lambda: g.iota(ap(R("offi")), [[16, 8]], -16, 0))
    iota(R("d0f"), [[0, 640]], 1024, 0)
    for n in ("frf", "frb"):
        iota(R(n, 0, 64), [[0, 64]], 0, 0)
        iota(R(n, 704, 736), [[0, 32]], 0, 0)
    iota(R("t1", 0, 16), [[0, 16]], 0, 0)
    iota(R("t1", 336, 352), [[0, 16]], 0, 0)
    iota(R("z01"), [[0, 320], [1, 2]], 0, 0)
    iota(R("d0b"), [[0, 640]], 1024, 0)
    iota(R("ac"), [[0, 32]], 0, 0)
    iota(R("bc"), [[0, 32]], 0, 0)
    iota(R("ones"), [[0, 512]], 1, 0)
    for b in range(4):
        o = R("et", 512 * b, 512 * b + 512)
        op("g", [o], [R("ones")], lambda o=o, b=b: g.affine_select(ap(o), ap(R("ones")), [[-1, 512]], A.is_equal, 0.0, b, 4))
    bits("ki", 15, A.bitwise_and)
    bits("si", 4, A.arith_shift_right, 1, A.bitwise_and)
    bits("p31", 31, A.bitwise_and)
    copy(one("kf"), one("ki"))
    copy(one("mo"), one("si"))
    copy(one("p31f"), one("p31"))
    ts(one("hh"), one("kf"), 15.0, A.is_lt, 512.0, A.mult)
    ts(R("df"), R("j16"), one("kf"), A.subtract)
    ts(R("k16"), R("ie"), 0.0, A.mult, one("kf"), A.add)
    ts(R("ha"), R("df"), 0.0, A.is_equal, -4096.0, A.mult)
    ts(R("hb"), R("df"), 1.0, A.is_equal, 512.0, A.mult)
    ts(R("iwc"), R("ie"), one("kf"), A.add, 160.0, A.subtract)
    tt(R("hc16"), R("ha"), R("hb"), A.add)
    pick("s", R("hc"), R("hc16"), R("k16"))
    for n, c, v in (("tw1", 0, -512.0), ("tw2", 0, 512.0)):
        fill(R(n, 0, 1), v)
        fill(R(n, 1, 16), -v)
    for n, a, b in (("s1", -1.0, 2.0), ("b1", 511.0, 385.0), ("s2", 1.0, 1.0), ("b2", -543.0, 928.0), ("gg", -16.0, 1264.0), ("sgo", -16.0, 176.0)):
        ts(one(n), one("mo"), a, A.mult, b, A.add)

    copy(R("qo16"), R("gqs"))
    copy(R("mo16"), R("gms"))
    pick("v", R("qr"), R("iot"), R("qo16"))
    ts(R("qf"), R("gqs"), 160.0, A.subtract)
    ts(R("mf"), R("gms"), 160.0, A.subtract)
    pick("v", R("qmr"), R("qr"), R("mo16"))
    tt(R("kw"), R("iwc"), R("mf"), A.min)
    copy(R("offu"), R("offi"))
    unrow("qmw", "qmr")
    fill(R("offu", 0, 1), 112)
    quant("uq", R("ut"), 0, 128)
    ts(R("kof"), R("kw"), 160.0, A.add)
    op("s", [R("uss")], [R("uqs"), R("offu")], lambda: g.scalar.activation(T.uss[:, 0:128], T.uqs[:, 0:128].indirect(T.offu[:, 0:8]), F.Copy))

    def tables(d, qw, qmw):
        tt(R("tiw"), R(qmw), R(qw), A.is_gt)
        tt(R("hiw"), R(qw), R(qmw), A.max)
        tt(R("low"), R(qw), R(qmw), A.min)
        copy(R("ti" + d), R("tiw"))
        ts(R("hi" + d), R("hiw"), 160.0, A.add)
        ts(R("lof" if d == "f" else "kob"), R("low"), 160.0, A.add)
        pick("s", R("t" + d), R("tw1"), R("ti" + d))
        pick("v" if d == "f" else "s", R("d1" + d, 1, 640, 2), R("iot"), R("hi" + d))
        pick("s", R("d0" + d, 1, 640, 2), R("iot"), R("lof" if d == "f" else "kob"))

    def window_list(d, kw):
        ts(R("kta"), R("tiw"), -320.0, A.mult, 480.0, A.add)
        tt(R("ktc"), R("kta"), R(kw), A.add)
        copy(R("kt" + d), R("ktc"))

    def signs(moving, h):
        c0, c1 = HALVES[h]
        mx(h, c1 - c0, "us", 0, moving, c0)
        act(R("sg", c0, c1), R("ps%d" % h, 0, c1 - c0), F.Sign, bias=-EPS)

    def halves(name, src, decide):
        for h, (c0, c1) in enumerate(HALVES):
            quant(name, R(src, 4 * c0, 4 * c1), c0, c1)
            if decide:
                signs(name, h)

    op("v", [R("usc")], [R("uqc"), R("offu")], lambda: g.vector.tensor_copy(T.usc[:, 0:128].bitcast(dt.uint32), T.uqc[:, 0:128].bitcast(dt.uint32).indirect(T.offu[:, 0:8])))
    tables("f", "qf", "qmw")
    halves("xq", "xt", True)
    pick("s", R("mr"), R("iot"), R("mo16"))

    def ring():
        state["bank"] += 1
        return 2 + state["bank"] % 6

    def choose(d):
        pick_tt(R("d1" + d, 0, 640, 2), R("sg"), R("ko" + d), R("t" + d), A.mult)

    def rows(d):
        scan(R("fr" + d, 64, 704), R("d0" + d), R("d1" + d), A.max, A.min)

    def place(kind, out, s, p0=0, p1=128):
        if kind in "12":
            ts(out, s, one("s" + kind, p0, p1), A.mult, one("b" + kind, p0, p1), A.add)
        else:
            ts(out, s, one(kind, p0, p1), A.add)

    def lists(d, q, s, p0, p1, with_sl):
        sl, ll = ("sl", "ll") if d == "f" else ("slb", "llb")
        p = (32 * q, 32 * q + p1 - p0)
        todo = [lambda: place("1" if d == "f" else "gg", R(ll, 0, 20, 2, *p), s, p0, p1), lambda: place("gg" if d == "f" else "2", R(ll, 1, 20, 2, *p), s, p0, p1)]
        one_more = lambda: place("sgo", R(sl, 0, 10, 1, *p), s, p0, p1)
        for f in ([one_more] if with_sl == 1 else []) + todo + ([one_more] if with_sl == 2 else []):
            f()

    def turned(q, st):
        return R("tt", 0, 10 * st, st, 32 * q, 32 * q + 32), 32 * q, 32 * q + 32

    def step(d, q, to, with_sl):
        pick("v", R("rr"), R("fr" + d, 1088, 1440), R("sl" if d == "f" else "slb"))
        spare()
        turn(R("tt", 0, 160, 1, 32 * q, 32 * q + 32), R("rr", 0, 160, 1, 32 * q, 32 * q + 32))
        spare()
        lists(d, to, *turned(q, 16), with_sl)

    def finish(d, out, crossed):
        pick("v", R("mm"), R("fr" + d), R("ll" if d == "f" else "llb"))
        spare()
        turn(R("tm"), R("mm"))
        spare()
        ts(R(out), R("tm", 0, 320, 16), 160.0, A.add)
        spare()
        for q in crossed:
            p = (32 * q, 32 * q + 32)
            ts(R(out, 1, 20, 4, *p), R("tm", 32, 320, 64, *p), 160.0, A.add)
            ts(R(out, 2, 20, 4, *p), R("tm", 16, 320, 64, *p), 160.0, A.add)

    def compose(d, between):
        fr, o = "fr" + d, 0 if d == "f" else 16
        turn(R("t1", 16, 336), R(fr, 65, 704, 2))
        turn(R("t1p"), R(fr, 33, 736, 2))
        turn(R(fr, 736, 1088), R("t1"))
        k = "2" if d == "f" else "1"
        place(k, R("fl", 0, 22, 2), R("t1p", o, 352, 32))
        place(k, R("fl", 1, 20, 2), R("t1", 16 + o, 336, 32))
        between()
        pick("v", R(fr, 1088, 1440), R(fr, 0, 1088), R("fl"))
        spare()

    def planes(src):
        for t in range(4):
            act(R("xp", C * t, C * t + C), R(src, t, 1280, 4), F.Copy, scale=0.5)
            act(R("xi", C * t, C * t + C) if t < 3 else R("ys", 0, 640, 2), R(src, t, 1280, 4), F.Copy, scale=0.5)

    def passes(out, win, off, other, pairs, between):
        def fused(t):
            pick_tt(R(out, t, 1280, 4), R(win, C * t, C * t + C), R(off), other(t), A.add)
        pick("s", R(pairs, 1, 640, 2), R(win, 960, 1280), R(off))
        fused(0)
        between[0]()
        scan(R(out, 1, 1280, 2), R("z01"), R(pairs), A.mult, A.add)
        between[1]()
        fused(2)
        fused(1)

    ts(R("vf"), R("ie", 0, 10), 2.0, A.mult, one("p31f"), A.add)
    fill(R("fl", 20, 22), 0)
    ts(R("vf"), R("vf"), 160.0, A.subtract)
    lists("f", 0, R("vf"), 0, 128, 1)
    window_list("f", "kw")
    waiting += [
        lambda: op("v", [R("qir")], [R("qo16"), R("iot")], lambda: g.vector.tensor_copy(ap(R("qir")).indirect(ap(R("qo16"))), ap(R("iot")))),
        lambda: unrow("qiw", "qir"),
        lambda: ts(R("qio"), R("qiw"), 160.0, A.add),
        lambda: (pick("s", R("mqr"), R("mr"), R("qio")), planes("xt")),
        lambda: lists("b", 0, R("vf"), 0, 128, 1),
        lambda: copy(R("ac", 0, 20), R("iwc")),
        lambda: unrow("mqw", "mqr"),
        lambda: turn(R("at"), R("ac")),
        lambda: tables("b", "qiw", "mqw"),
        lambda: copy(R("a2", 0, 16, 1, 0, 32), R("at", 0, 16, 1, 0, 32)),
        lambda: window_list("b", "low")]

    def nothing():
        pass

    for rnd, s in enumerate(ROUNDS):
        peer = T.cores[rank ^ s]
        rid, pid, _se = topo.addr(peer)
        mask, neng = topo.mask(core, peer), len(topo.engines(core, peer))
        choose("f")
        spare()
        rows("f")
        spare()
        compose("f", spare)
        turn(R("tt", 0, 320, 1, 0, 32), R("frf", 1104, 1424, 1, 0, 32))
        spare()
        lists("f", 1, *turned(0, 32), 1)
        step("f", 1, 2, 1)
        step("f", 2, 3, 2)
        finish("f", "xo", (2,))
        while waiting:
            spare()
        passes("vt", "xp", "xo", lambda t: R("xi", C * t, C * t + C), "ys", (nothing, nothing))
        halves("vq", "vt", True)
        for h, (c0, c1) in enumerate(HALVES):
            for b in range(4):
                k = ring()
                mx(k, c1 - c0, "wq", 128 * b, "vq", c0)
                act(R("ht", 4 * c0 + b, 4 * c1, 4), R("ps%d" % k, 0, c1 - c0), F.Copy, scale=0.03125)
        act(R("yv", 0, 640, 2), R("vt", 3, 1280, 4), F.Copy)
        pick("v", R("rr8"), R("frf", 1088, 1440), R("sl"))
        ts(R("ac", 0, 20), R("xo"), 160.0, A.subtract)
        turn(R("tt", 0, 160, 1, 96, 128), R("rr8", 0, 160, 1, 96, 128))
        turn(R("at"), R("ac"))
        lists("b", 3, *turned(3, 16), 1)
        if rnd == 0:
            quant("vvq", R("vv"), 0, 128)
        waiting.append(lambda: copy(R("a2", 16, 32), R("at", 0, 16)))
        waiting += [lambda q=q: copy(R("a2", 0, 16, 1, 32 * q + 32, 32 * q + 64), R("at", 16, 32, 1, 32 * q, 32 * q + 32)) for q in range(3)]

        def send(h):
            c0, c1 = C * rnd + HALVES[h][0], C * rnd + HALVES[h][1]
            quant("hq", R("ht", 4 * HALVES[h][0], 4 * HALVES[h][1]), c0, c1)
            order("g", [], [R("hqc", c0, c1), R("hqs", c0, c1)])
            sem = "ar%d_%d" % (rnd, h)
            g.remote_dma(T.rqc[:, c0:c1].bitcast(dt.uint8), T.hqc[:, c0:c1].bitcast(dt.uint8), T.sem[sem], T.sem.lsem, pid, rid, mask)
            g.remote_dma(T.rqs[:, c0:c1], T.hqs[:, c0:c1], T.sem[sem], T.sem.lsem, pid, rid, mask)
            pending["lsem"] = pending.get("lsem", 0) + 2 * neng
            pending[sem] = 2 * neng
            clock[(sem, 2 * neng)] = {}
            note([R("rqc", c0, c1), R("rqs", c0, c1)], [], (sem, 2 * neng))

        choose("b")
        spare()
        rows("b")
        send(0)
        compose("b", lambda: send(1))
        step("b", 3, 2, 1)
        step("b", 2, 1, 1)
        if rnd == 0:
            quant("eq", R("et"), 0, 512)
        step("b", 1, 0, 0)
        for h, (c0, c1) in enumerate(HALVES):
            for b in range(4):
                k = ring()
                mx(k, c1 - c0, "eq", 128 * b, "rq", C * rnd + c0)
                act(R("dp", C * b + c0, C * b + c1), R("ps%d" % k, 0, c1 - c0), F.Copy)
        finish("b", "xob", (1, 3))
        while waiting:
            spare()
        xn = "xn%d" % rnd
        last = rnd == 2

        def misses():
            cu, old = "cu%d" % (rnd % 2), "cu%d" % (1 - rnd % 2)
            tt(R("md" if rnd else cu), R("a2"), R("bt"), A.not_equal)
            if rnd:
                tt(R(cu), R(old), R("md"), A.not_equal)
            turn(R("cut"), R(cu))
            copy(R("moff"), R("cut"))
            a, b = (320, 0) if last else (0, 320)
            pick("s", R("w", a, a + 320), R("tw2"), R("moff", 0, 20))
            act(R("w", b, b + 320), R("w", a, a + 320), F.Copy, scale=-1.0)
            pick("s", R("d1f", 0, 640, 2) if last else R("tf"), R("w"), R("ktf"))
        ts(R("bc", 0, 20), R("xob"), 160.0, A.subtract)
        passes(xn, "dp", "xob", lambda t: R("vt", t, 1280, 4), "yv", (lambda: turn(R("bt"), R("bc")), misses))
        halves("xq", xn, not last)
        if not last:
            planes(xn)
            pick("s", R("tb"), R("w"), R("ktb"))

    for h, (c0, c1) in enumerate(HALVES):
        mx(h, c1 - c0, "vvq", 0, "xq", c0)
        copy(R("yt", c0, c1), R("ps%d" % h, 0, c1 - c0))
        dma("y", [], [R("yt", c0, c1)], T.y[:, c0:c1], ap(R("yt", c0, c1)))
    rows("f")
    act(R("qout"), R("frf", 65, 704, 2), F.Identity, bias=160.0)
    dma("s", [], [R("qout")], T.qo[:, :], T.qout[0:128:16, :])
    dma("y", [], [R("xqc")], T.oc[:, :], T.xqc[:, :].bitcast(dt.uint8))
    for k in range(4):
        dma("y", [], [R("xqs")], T.osc[4 * k:4 * k + 4, :], T.xqs[32 * k:32 * k + 4, :])
    for sem, val in sorted(pending.items()):
        g.wait_ge(T.sem[sem], val)
    for sem, val in count.items():
        g.wait_ge(T.sem[sem], val)
